import numpy as np, ml_dtypes
CORES = [40,41,42,43,44,45,46,47]
N = 8
BF = ml_dtypes.bfloat16
V, S, Q, RO, W = 1024, 4, 256, 6, 2304
def pack(res, cap, B, T, K, wt, ka):
    w = B + 4096 * T - 65536 * K
    return {"res": np.ascontiguousarray(res).reshape(N, 128, W).astype(np.float32).astype(BF), "cap": np.ascontiguousarray(cap).reshape(N, 128, V).astype(np.float32).astype(BF),
            "br": np.ascontiguousarray(w).reshape(N, 128, V).astype(np.int32), "wt": np.ascontiguousarray(wt).reshape(N, 128, 1).astype(np.int32), "ka": np.ascontiguousarray(ka).reshape(N, 128, 1).astype(np.int32)}
def parts(rng):
    sh = (N, 8, 16, V)
    res = (rng.integers(4, 29, (N, 8, 1, W)) * rng.random((N, 8, 16, W))).astype(np.int64)
    heavy = (rng.random((N, 8, 1, W)) < 0.06) & (rng.random((N, 8, 16, W)) < 0.7)
    res = np.where(heavy, rng.integers(0, 256, res.shape), res)
    cap = rng.integers(0, 64, sh); dead = rng.choice(np.array([0.0, 0.25, 0.5]), (N, 8, 1, 1))
    B = rng.integers(0, W, sh); T = np.where(rng.random(sh) < dead, 0, rng.integers(0, 16, sh)); K = np.where(rng.random(sh) < 0.5, 0, rng.integers(0, 16, sh))
    return res, cap, B, T, K, rng.integers(0, 256, (N, 8, 16, 1)), rng.integers(0, V, (N, 8, 16, 1))
def setup_inputs(rng):
    return pack(*parts(rng))
def setup_inputs_corners(rng):
    res, cap, B, T, K, wt, ka = parts(rng)
    v = np.arange(V); t0 = v % S + 1; row = np.arange(16).reshape(16, 1)
    res[..., W - 16:] = np.where(row < np.arange(16), 200, 0)
    res[:, 5, :, 0:V:2] = 255; res[:, 6, :, 0:V:2] = 0; cap[:, 6, :, ::2] = 63
    cl = rng.integers(0, 9, (N, 8, 1, V)); one = rng.integers(0, 16, (N, 8, 1, V)); near = W - 16 + rng.integers(3, 7, (N, 8, 1, V)); same = rng.integers(0, W, (N, 8, 1, V))
    T = np.where(cl == 0, t0 - 1, T); K = np.where(cl == 0, 0, K)
    T = np.where(cl == 1, 15, T); K = np.where(cl == 1, 0, K)
    T = np.where(cl == 2, np.where(row % 2 == 0, t0, t0 - 1), T); K = np.where(cl == 2, 0, K)
    T = np.where(cl == 3, 15, T); K = np.where(cl == 3, np.where(row % 2 == 0, t0 - 1, t0), K)
    T = np.where(cl == 4, np.where(row == one, 15, 0), T); K = np.where(cl == 4, 0, K); B = np.where(cl == 4, near, B); cap = np.where(cl == 4, 63, cap)
    T = np.where(cl == 5, 15, T); K = np.where(cl == 5, 0, K); B = np.where(cl == 5, same, B)
    cap = np.where(cl == 5, np.minimum(np.take_along_axis(res, same, 3), 63), cap)
    chain = np.where(row == 0, v, np.where(row == 1, np.maximum(v - 1, 0), np.where(row == 2, W - 1, np.where(row == 3, 0, V))))
    T = np.where(cl == 6, np.where(row < 5, 15, 0), T); K = np.where(cl == 6, 0, K); B = np.where(cl == 6, chain, B)
    two = (cl == 7) & ((row == 3) | (row == 15))
    T = np.where(two, 15, T); K = np.where(two, 0, K); B = np.where(two, near, B); cap = np.where(cl == 7, 63, cap)
    q = rng.permutation(N); T[q[0], 7] = 0; T[q[1], 7] = 15; K[q[1], 7] = 0
    wt[:, 0] = 0; wt[:, 1] = 255; ka[:, 2] = 0; ka[:, 3] = V - 1; ka[:, 4] = rng.choice(np.array([0, V >> 1]), (N, 16, 1))
    return pack(res, cap, B, T, K, wt, ka)
def setup_inputs_ends(rng):
    sh = (N, 8, 16, V); lane = np.arange(16).reshape(16, 1)
    kd = rng.choice(6, (N, 8, 1, W), p=[0.38, 0.12, 0.25, 0.1, 0.08, 0.07])
    kd[:, :, 0, W - 1] = np.where(np.arange(8) % 2 == 1, 1, 2); kd[:, 7, 0, V - 1] = 5; kd[:, 7, 0, V - 2] = 4
    rot = (lane + rng.integers(0, 16, (N, 8, 1, W))) % 16; some = 255 * (rng.random((N, 8, 16, W)) < 0.2)
    res = np.where(kd == 1, 255, np.where(kd == 2, some, np.where(kd == 3, 63, np.where(kd == 4, np.where(rot < 4, 255, 63), np.where(kd == 5, np.where(rot < 5, 255, 63), 0)))))
    ck = rng.choice(3, (N, 8, 1, V), p=[0.5, 0.15, 0.35]); cap = np.where(ck == 0, 63, np.where(ck == 1, 0, 63 * rng.integers(0, 2, sh)))
    up = rng.random(sh) < rng.choice(np.array([0.0, 0.1, 0.2]), (N, 8, 1, V))
    B = np.where(up, W - 1, 0); T = np.where(up, 15, 0); K = np.where(up, 0, 15)
    fr = rng.random(sh) < rng.choice(np.array([0.0, 0.1, 0.2, 0.4]), (N, 8, 1, V)); live = rng.random(sh) < 0.8
    B = np.where(fr, np.where(rng.random(sh) < 0.7, rng.integers(0, W, sh), rng.choice(np.array([0, V - 1, V, W - 1]), sh)), B)
    T = np.where(fr, np.where(live, 15, 15 * rng.integers(0, 2, sh)), T); K = np.where(fr, np.where(live, 0, 15 * rng.integers(0, 2, sh)), K)
    for j, first, col, c in ((0, 15, V - 1, 63), (1, 15, V - 2, 63), (2, 14, W - 1, 0)):
        a = S * (Q - 1 - j)
        B[:, 7, :, a:a + S] = 0; T[:, 7, :, a:a + S] = 0; K[:, 7, :, a:a + S] = 15; cap[:, 7, :, a:a + S] = c
        B[:, 7, first:, a:a + S] = col; T[:, 7, first:, a:a + S] = 15; K[:, 7, first:, a:a + S] = 0
    wt = np.where(rng.random((N, 8, 16, 1)) < 0.8, 255 * rng.integers(0, 2, (N, 8, 16, 1)), rng.integers(0, 256, (N, 8, 16, 1))); wt[:, 7] = 255; wt[:, 0, 0] = 0
    ka = np.where(rng.random((N, 8, 16, 1)) < 0.8, (V - 1) * rng.integers(0, 2, (N, 8, 16, 1)), rng.integers(0, V, (N, 8, 16, 1)))
    ka[:, 7] = rng.integers(0, V, (N, 16, 1)); ka[:, 0, 0] = 0; ka[:, 0, 1] = V - 1; ka[:, 7, 15] = V - 1
    return pack(res, cap, B, T, K, wt, ka)
def setup_inputs_full(rng):
    res, cap, B, T, K, wt, ka = parts(rng); q = rng.permutation(N); i = np.arange(Q); lane = np.arange(16).reshape(16, 1)
    res[..., W - 16:] = np.where(lane < np.arange(16), 200, 0)
    a = q[0]; T[a, :, :, 0::S] = 0; T[a, :, :, 1::S] = 0; cap[a, :, :, 1::S] = 63
    odd = rng.permutation(8 * Q)[:2 * int(rng.integers(1, 100)) + 1]; k = rng.integers(0, 16, odd.size); g = odd // Q; v = S * (odd % Q)
    B[a, g, k, v] = W - 16 + rng.integers(6, 16, odd.size); T[a, g, k, v] = 15; K[a, g, k, v] = 0
    a = q[1]; hit = lane == rng.integers(0, 16, (8, 1, Q))
    B[a, :, :, 0::S] = np.where(hit, W - 16 + rng.integers(6, 16, (8, 1, Q)), B[a, :, :, 0::S]); T[a, :, :, 0::S] = np.where(hit, 15, T[a, :, :, 0::S]); K[a, :, :, 0::S] = np.where(hit, 0, K[a, :, :, 0::S])
    for a, s in ((q[0], 2), (q[1], 1)):
        five = rng.random((8, 1, Q)) < 0.6; hit = lane == rng.integers(0, 16, (8, 1, Q))
        B[a, :, :, s::S] = np.where(five & hit, W - 11, B[a, :, :, s::S]); K[a, :, :, s::S] = np.where(five & hit, 0, K[a, :, :, s::S])
        T[a, :, :, s::S] = np.where(five, np.where(hit, 15, 0), T[a, :, :, s::S])
    a = q[2]; T[a] = 15; K[a] = 0; B[a, 1::2] = rng.integers(V, W, (4, 16, V))
    for g in (0, 4):
        base = rng.integers(200, 249, 16); turn = (lane + rng.integers(0, 16, (1, Q - 16))) % 16
        res[a, g, :, W - Q:W - 16] = base[turn] + (lane < rng.integers(0, 8, (1, Q - 16)))
        B[a, g] = np.where(rng.random((1, V)) < 0.5, rng.integers(W - Q, W - 16, (16, V)), B[a, g])
    a = q[3]; r = (a + 1) % N; T[a, :, :, 0::S] = 0
    for g in range(8):
        x, y = rng.permutation(16)[:2]; wt[r, g] = 0; wt[r, g, x] = 16; wt[r, g, y] = 1
        if g != 3: ka[r, g] = int(ka[r, g, 0, 0])
        o = rng.permutation(4096); p = ((o * o >> 5) + int(ka[r, g, 0, 0]) * o) & (V - 1)
        first = rng.permutation(np.unique(p, return_index=True)[1]); n = (Q, 8, Q, 1, Q, 8, Q, 1)[g]
        s = (o[first[rng.permutation(Q) % n]] - 37 * i) & 4095; col = V + rng.permutation(Q); k = rng.integers(0, 16, Q)
        res[a, g, :, V:V + Q] = 0; res[a, g, x, col] = s >> 4; res[a, g, y, col] = s & 15
        B[a, g, k, S * i] = col; T[a, g, k, S * i] = 15; K[a, g, k, S * i] = 0
    return pack(res, cap, B, T, K, wt, ka)
def setup_inputs_spread(rng):
    res, cap, B, T, K, wt, ka = parts(rng)
    res = (np.exp2(8 * rng.random((N, 8, 1, W)) ** 3) * rng.random((N, 8, 16, W))).astype(np.int64)
    res = np.where(rng.random((N, 8, 1, W)) < 0.02, rng.integers(0, 256, res.shape), np.minimum(res, 255))
    cap = np.minimum((np.exp2(6 - 6 * rng.random((N, 8, 1, V)) ** 3) * rng.random(cap.shape)).astype(np.int64), 63)
    B = np.minimum((W * rng.random(B.shape) ** rng.choice(np.array([0.5, 1.0, 3.0]), (N, 8, 1, 1))).astype(np.int64), W - 1)
    wt = np.minimum(np.exp2(8 * rng.random(wt.shape)).astype(np.int64), 255)
    return pack(res, cap, B, T, K, wt, ka)
def setup_inputs_ties(rng):
    res, cap, B, T, K, wt, ka = parts(rng)
    lane = np.arange(16).reshape(16, 1); turn = (lane + rng.integers(0, 16, (N, 8, 1, W))) % 16
    res = np.where(turn < rng.integers(2, 4, (N, 8, 1, W)), 40, 0)
    cap = np.broadcast_to(rng.choice(np.array([0, 20, 20, 39, 40, 63]), (N, 8, 1, V)), cap.shape)
    live = rng.random(B.shape) < rng.choice(np.array([0.1, 0.2, 0.3]), (N, 8, 1, 1))
    T = np.where(live, 15, 0); K = np.where(live, 0, K)
    wt[:, ::2] = 1; ka[:, 1::2] = rng.choice(np.array([0, 1, V >> 1, V - 1]), (N, 4, 16, 1))
    return pack(res, cap, B, T, K, wt, ka)
def check_inputs(d):
    bad = []
    for k, lo, hi in (("res", 0, 255), ("cap", 0, 63), ("br", -983040, 63743), ("wt", 0, 255), ("ka", 0, V - 1)):
        v = np.asarray(d[k]).astype(np.float64)
        if not np.all((v >= lo) & (v <= hi) & (v == np.floor(v))): bad.append("range of " + k)
    if np.any((np.asarray(d["br"]).astype(np.int64) & 4095) >= W): bad.append("column numbers in br")
    return bad
def reference(res, cap, br, wt, ka):
    R = res.astype(np.float32).astype(np.int32).reshape(N, 8, 16, W); C = cap.astype(np.float32).astype(np.int32).reshape(N, 8, 16, V)
    b = np.array(br, dtype=np.int32).reshape(N, 8, 16, V); w = wt.astype(np.int64).reshape(N, 8, 16, 1); kf = ka.astype(np.int64).reshape(N, 8, 16, 1)
    A = [0] * N; row = np.arange(16).reshape(1, 16, 1); i = np.arange(Q)
    for t in range(1, RO + 1):
        v = S * i + (t - 1) % S; sent = []
        for r in range(N):
            x = b[r][:, :, v]; on = (((x >> 12) & 15) >= t) & (-(x >> 16) < t)
            c = C[r][:, :, v]; most = 4 + (A[r] & 1)
            pick = np.take_along_axis(R[r], (x & 4095).reshape(8, 1, 16 * Q), 2).reshape(8, 16, 16, Q) * on[:, None]
            m = np.max(pick, axis=2); fail = np.sum(m > c, axis=1) > most
            over = np.where(on, np.sum(np.maximum(pick - c[:, :, None], 0), axis=1), -1)
            gone = fail[:, None] & (row == np.argmax(over, axis=1)[:, None])
            m = np.max(pick * (~gone)[:, None], axis=2)
            m = np.where((np.sum(m > c, axis=1) > most)[:, None], 0, m)
            b[r][:, :, v] = np.where(gone, (x & 65535) - 65536 * (t + S), x)
            R[r][:, :, v] = m; A[r] = int(np.sum(fail)); sent.append(m)
        for r in range(N):
            m = sent[(r - 1 - (t - 1) % (N - 1)) % N]
            u = (np.sum(w[r] * m, axis=1) + 37 * i) & 4095
            p = ((u * u >> 5)[:, None] + kf[r] * u[:, None]) & (V - 1)
            slack = np.maximum(C[r] - R[r][:, :, :V], 0)
            sl = np.take_along_axis(slack, p.reshape(8, 1, 16 * Q), 2).reshape(8, 16, 16, Q)
            score = np.sum(np.minimum(m[:, :, None], sl), axis=1)
            par = np.take_along_axis(p, np.argmax(score, axis=1)[:, None], 1)[:, 0]
            for g in range(8):
                node, first = np.unique(par[g], return_index=True)
                b[r, g, first & 15, node] = V + Q * (t - 1) + first + 4096 * (t + 2)
            if t < RO: R[r][:, :, V + Q * (t - 1):V + Q * t] = m
    return {"yr": np.ascontiguousarray(R[..., :V]).reshape(N, 128, V).astype(np.float32).astype(BF), "yb": b.reshape(N, 128, V).astype(np.float32)}

@@ -1,0 +1,560 @@
+from concourse.mybir import AluOpType, ActivationFunctionType
+import comms_topo
+
+OP = AluOpType
+AF = ActivationFunctionType
+B16, F32, I32, U16 = "bfloat16", "float32", "int32", "uint16"
+ROUNDS, PH = 6, 4
+MV = 8
+SH = 16
+AREA0, AREAD = 13312, 4352
+RWN = AREA0 + AREAD * 4 + 256
+DDN = 4384
+
+SCRATCH = {}
+
+
+def _buf(where, dtype, *names):
+    for n in names:
+        SCRATCH[n[0]] = (where, [128, n[1]], dtype)
+
+
+_buf("sbuf", B16, ("RW", RWN), ("CAPS", 1024), ("SL", 1024), ("DD", DDN), ("E1", 4096), ("E2", 4096), ("X", 4096), ("SEG", 4096), ("TT", 256), ("FL", 256),
+     ("F2", 256), ("MN", 256), ("A1", 256), ("A2", 256), ("EX", 256), ("EXP", 256), ("JK", 256), ("MR", 1024), ("SG", 2048), ("EQ", 2176))
+_buf("sbuf", F32, ("W", 1280), ("BC", 1024), ("OFA", 256), ("OFB", 256), ("EQT", 256), ("DF", 256), ("T1", 256), ("EXD", 256), ("EXN", 256),
+     ("PBF", 256), ("SX", 256), ("S16F", 160), ("TW", 256), ("NW", 256))
+_buf("sbuf", I32, ("BRI", 1024), ("YL", 1024), ("KI", 256), ("S16I", 224), ("UI", 256), ("PI1", 256), ("PI2", 256), ("WTI", 1), ("KAI", 1), ("I1", 8))
+_buf("sbuf", U16, ("OFFS", 256), ("IDX", 16), ("POF", 256), ("PBU", 256), ("LST", 16), ("LSD", 16), ("LID", 16), ("LLN", 16))
+_buf("sbuf", B16, ("IB", 256), ("IB15", 256), ("IB4", 256), ("MSKD", 256), ("NEGM", 256), ("BB", 128), ("BB4", 128), ("WB", 128), ("O8K", 8), ("O8S", 8), ("O8N", 8), ("O8M", 8), ("O8W", 8),
+     ("BSM", 128), ("ID", 128), ("IDN", 128), ("CK", 256), ("ONE", 128), ("C37", 128), ("ZR", 256))
+_buf("sbuf", F32, ("F1", 24), ("NMSK", 256), ("TRIM", 256), ("SEGM", 256), ("KR", 256), ("KAX", 256), ("BBF", 128), ("O8F", 8), ("CIX", 16), ("TRX", 16), ("TRD", 16), ("IDF", 128), ("O16", 128), ("NWN", 256))
+SCRATCH.update({"KRW": ("sbuf", [2, 128], I32), "KH": ("sbuf", [2, 128], I32), "KL": ("sbuf", [2, 128], I32), "KHF": ("sbuf", [2, 128], F32), "KLF": ("sbuf", [2, 128], F32), "KC": ("sbuf", [2, 256], B16)})
+_buf("psum", F32, ("pk", 512), ("pb", 512), ("pn", 512), ("pc", 512), ("pd", 2048))
+for _f in range(PH):
+    _buf("sbuf", B16, ("CX%d" % _f, 4096))
+for _r in range(1, ROUNDS + 1):
+    _buf("sbuf", B16, ("MO%d" % _r, 256), ("LD%d" % _r, 256))
+ALIAS = {n: ("F1", c, 1) for c, n in enumerate(("PIF", "LNF", "GRF", "LREV", "LN16", "OMP", "WTF", "KAF", "LIM", "FC", "SC", "H1", "H2", "LP0", "LP1", "LP2", "LP3"))}
+ALIAS.update({n: ("I1", c, 1) for c, n in enumerate(("PIX", "LNI", "GRI"))})
+ALIAS.update({n: ("S16I", 16 * c, 16) for c, n in enumerate(("TA", "TB", "U", "U2", "BS", "P2", "PL", "UT0", "UT", "UT2", "BST", "PLI", "PL3"))})
+ALIAS.update({n: ("S16F", 16 * c, 16) for c, n in enumerate(("TAF", "P1", "PLF", "L1", "L2", "L3", "L4", "PZ", "PQ"))})
+PSUM = ("pk", "pb", "pn", "pc", "pd")
+LOADS = ["lcap", "lbr", "lres", "lwt", "lka", "lk0", "lk1"]
+SEMAPHORES = ["sV", "sS", "sP", "sG", "sent", "oyr", "oyb"] + LOADS + ["arr%d" % r for r in range(1, ROUNDS + 1)]
+
+
+def scheduler(g, T):
+    eng = {"V": g.vector, "S": g.scalar, "P": g.tensor, "G": g, "Y": g.sync}
+    cnt, rec, snap = {}, {}, {}
+    clk = {q: {} for q in eng}
+
+    def ref(name, a=None, b=None, s=1, p=None):
+        if name in ALIAS:
+            name, o, w = ALIAS[name]
+            a, b = o + (a or 0), o + (w if b is None else b)
+        a = 0 if a is None else a
+        b = SCRATCH[name][1][1] if b is None else b
+        if s > 0:
+            sl = slice(a, b, s)
+        else:
+            sl = slice(b - 1, a - 1 if a else None, -1)
+        rows = slice(0, p) if p else slice(0, SCRATCH[name][1][0])
+        x = (name, a, b, max(s, 1), a % max(s, 1))
+        return {"ap": T[name][rows, sl], "r": [x], "w": [x]}
+
+    def ind(win, off):
+        return {"ap": win["ap"].indirect(off["ap"]), "r": win["r"] + off["r"], "w": win["w"], "x": off["r"]}
+
+    def overlap(q, x, y):
+        if x[0] in PSUM and q:
+            return x[1] // 512 <= (y[2] - 1) // 512 and y[1] // 512 <= (x[2] - 1) // 512
+        if x[3] == y[3] and x[4] != y[4]:
+            return False
+        return x[1] < y[2] and y[1] < x[2]
+
+    def deps(q, reads, writes):
+        need = {}
+        for isw, rs in ((False, reads), (True, writes)):
+            for x in rs:
+                for (y, w, q2, n) in rec.get(x[0], []):
+                    same = q2 == q
+                    if not overlap(not same, x, y) or (same and q == "P"):
+                        continue
+                    if not (w or isw or (x[0] in PSUM and not same)):
+                        continue
+                    if need.get(q2, 0) < n:
+                        need[q2] = n
+        for q2 in sorted(need):
+            n = need[q2]
+            if clk[q].get(q2, 0) >= n:
+                continue
+            if any(q3 != q2 and snap.get((q3, m), {}).get(q2, 0) >= n for q3, m in need.items() if clk[q].get(q3, 0) < m):
+                continue
+            eng[q].wait_ge(T.sem["s" + q2] if q2 in eng else T.sem[q2], n)
+        for q2, n in need.items():
+            if clk[q].get(q2, 0) < n:
+                clk[q][q2] = n
+                for q3, m in snap.get((q2, n), {}).items():
+                    if clk[q].get(q3, 0) < m:
+                        clk[q][q3] = m
+
+    def record(q, n, reads, writes, by):
+        s = dict(clk[by]) if by else {}
+        if q in eng:
+            s[q] = max(s.get(q, 0), n - 1)
+        snap[(q, n)] = s
+        for x in writes:
+            rec[x[0]] = [e for e in rec.get(x[0], []) if not (x[1] <= e[0][1] and e[0][2] <= x[2] and (x[3] == 1 or x[3:] == e[0][3:]))]
+        for w, rs in ((False, reads), (True, writes)):
+            for x in rs:
+                rec.setdefault(x[0], []).append((x, w, q, n))
+
+    def op(q, fn, outs, ins):
+        reads = [x for i in ins for x in i["r"]] + [x for o in outs for x in o.get("x", [])]
+        writes = [x for o in outs for x in o["w"]]
+        deps(q, reads, writes)
+        cnt[q] = cnt.get(q, 0) + 1
+        fn().then_inc(T.sem["s" + q], 1)
+        record(q, cnt[q], reads, writes, q)
+
+    def dma(q, sem, out, in_, outs, ins):
+        reads, writes = [x for i in ins for x in i["r"]], [x for o in outs for x in o["w"]]
+        deps(q, reads, writes)
+        eng[q].dma_start(out, in_).then_inc(T.sem[sem], 16)
+        record(sem, 16, reads, writes, q)
+
+    return {"ref": ref, "ind": ind, "op": op, "dma": dma, "deps": deps, "record": record, "cnt": cnt}
+
+
+def rank_program(g, core, T, topo):
+    rank = T.rank_of(core)
+    if rank is None:
+        return
+    sc = scheduler(g, T)
+    R, IND, op = sc["ref"], sc["ind"], sc["op"]
+
+    def val(x):
+        return x["ap"] if isinstance(x, dict) else x
+
+    def tt(out, a, b, o):
+        op("V", lambda: g.vector.tensor_tensor(out["ap"], a["ap"], b["ap"], o), [out], [a, b])
+
+    def ts(out, a, s1, s2, o0, o1=None):
+        ins = [a] + [s for s in (s1, s2) if isinstance(s, dict)]
+        if o1 is None:
+            op("V", lambda: g.vector.tensor_scalar(out["ap"], a["ap"], val(s1), None, o0), [out], ins)
+        else:
+            op("V", lambda: g.vector.tensor_scalar(out["ap"], a["ap"], val(s1), val(s2), o0, o1), [out], ins)
+
+    def cp(out, a):
+        op("V", lambda: g.vector.tensor_copy(out["ap"], a["ap"]), [out], [a])
+
+    def scan(out, d0, d1, o0, o1):
+        op("V", lambda: g.vector.tensor_tensor_scan(out["ap"], d0["ap"], d1["ap"], 0.0, o0, o1), [out], [d0, d1])
+
+    def ms(out, v):
+        op("V", lambda: g.vector.memset(out["ap"], v), [out], [])
+
+    def act(out, a, f, scale=1.0, bias=0.0, acc=None):
+        ins = [a] + [v for v in (scale, bias) if isinstance(v, dict)]
+        if acc:
+            op("S", lambda: g.scalar.activation(out["ap"], a["ap"], f, bias=val(bias), scale=val(scale), accum_out=acc["ap"]), [out, acc], ins)
+        else:
+            op("S", lambda: g.scalar.activation(out["ap"], a["ap"], f, bias=val(bias), scale=val(scale)), [out], ins)
+
+    def aff(out, a, scale, bias=0.0):
+        act(out, a, AF.Identity, scale, bias)
+
+    def mm(out, l, r, start, stop):
+        op("P", lambda: g.tensor.matmul(out["ap"], l["ap"], r["ap"], start, stop), [out], [l, r])
+
+    def iota(out, pattern, base, cm):
+        if SCRATCH[out["r"][0][0]][2] == I32:
+            op("G", lambda: g.iota(out["ap"], pattern, base, cm), [out], [])
+        else:
+            op("G", lambda: g.iota(out["ap"], pattern, base, cm, allow_small_or_imprecise_dtypes=True), [out], [])
+
+    def gcopy(a, b, n):
+        op("G", lambda: g.affine_select(a["ap"], b["ap"], [[0, n]], OP.is_gt, 0.0, 1, 0), [a], [b])
+
+    def widen(f, k, q, h=None):
+        if h is None:
+            a, b = R("CX%d" % f, k, 4096, 16), R("CAPS", f, 1024, 4)
+        else:
+            a, b = R("CX%d" % f, 2048 * h + k, 2048 * h + 2048, 16), R("CAPS", 512 * h + f, 512 * h + 512, 4)
+        if q == "G":
+            gcopy(a, b, 256 if h is None else 128)
+        elif q == "V":
+            cp(a, b)
+        else:
+            act(a, b, AF.Copy)
+
+    sc["dma"]("Y", "lbr", R("BRI")["ap"], T.br[:], [R("BRI")], [])
+    sc["dma"]("S", "lcap", R("CAPS")["ap"], T.cap[:], [R("CAPS")], [])
+    x = R("RW", SH, SH + 2304)
+    sc["dma"]("Y", "lres", x["ap"], T.res[:], [x], [])
+    sc["dma"]("S", "lwt", R("WTI")["ap"], T.wt[:], [R("WTI")], [])
+    sc["dma"]("S", "lka", R("KAI")["ap"], T.ka[:], [R("KAI")], [])
+    for p in (0, 1):
+        g.scalar.dma_start(T.KRW[p:p + 1, :], T.ka[:]).then_inc(T.sem["lk%d" % p], 16)
+        sc["record"]("lk%d" % p, 16, [], [("KRW", p, p + 1, 1, 0)], "S")
+
+    iota(R("PIX"), [[0, 1]], 0, 1)
+    iota(R("IB15"), [[0, 16], [1, 16]], 0, 0)
+    iota(R("IB4"), [[1, 16], [0, 16]], 0, 0)
+    iota(R("IB"), [[1, 256]], 0, 0)
+    for k in range(4):
+        widen(0, k, "G", 1)
+    iota(R("CIX"), [[256, 16]], 15, 0)
+    iota(R("TRX"), [[16, 16]], 1024, 0)
+    iota(R("TRD"), [[16, 16]], 4128, 0)
+    iota(R("NWN"), [[1, 256]], AREA0 - AREAD, 0)
+    ms(R("RW", 0, SH), 0.0)
+    ms(R("DD", 0, 16), 0.0)
+    ms(R("DD", 4112, DDN), 0.0)
+    ms(R("LIM"), 4.0)
+    ms(R("ONE"), 1.0)
+    ts(R("LNI"), R("PIX"), 15, None, OP.bitwise_and)
+    ts(R("GRI"), R("PIX"), 4, None, OP.arith_shift_right)
+    cp(R("PIF"), R("PIX"))
+    cp(R("LNF"), R("LNI"))
+    cp(R("GRF"), R("GRI"))
+    ts(R("SEG", 0, 256), R("IB15"), 0.0, 768.0, OP.is_gt, OP.mult)
+    ts(R("SEG", 0, 256), R("SEG", 0, 256), -256.0, None, OP.add)
+
+    def halves(f):
+        ts(R("YL", f, 1024, 4), R("BRI", f, 1024, 4), 65535, None, OP.bitwise_and)
+        ts(R("KI"), R("BRI", f, 1024, 4), 4095, None, OP.bitwise_and)
+        ts(R("BC", 256 * f, 256 * f + 256), R("KI"), float(SH), None, OP.add)
+
+    def code(f, t, out, q):
+        a, b = (R("pn", 0, 256), R("pc", 0, 256)) if q == "V" else (R("MN"), R("A1"))
+        ts(a, R("BRI", f, 1024, 4), float(-65536 * (t - 1)), -8192.0, OP.is_lt, OP.mult)
+        ts(b, R("YL", f, 1024, 4), float(4096 * t), -8192.0, OP.is_lt, OP.mult)
+        bc = R("BC", 256 * f, 256 * f + 256)
+        if q == "V":
+            tt(R("DF"), bc, a, OP.add)
+            tt(out, R("DF"), b, OP.add)
+        else:
+            s = R("pd", 512 * q, 512 * q + 256)
+            mm(s, R("IDF"), bc, True, False)
+            mm(s, R("ID"), a, False, False)
+            mm(s, R("ID"), b, False, True)
+            act(out, s, AF.Copy)
+    for n in (256, 512):
+        act(R("SEG", n, 2 * n), R("SEG", 0, n), AF.Copy)
+    for n in (1024, 2048):
+        gcopy(R("SEG", n, 2 * n), R("SEG", 0, n), n)
+    for k in range(4, 16):
+        widen(0, k, "S", 1)
+    for k in range(11, 16):
+        widen(0, k, "S", 0)
+    halves(0)
+    code(0, 1, R("W", 0, 1024, 4), "V")
+    cp(R("OFFS"), R("W", 0, 1024, 4))
+    for k in range(11):
+        widen(0, k, "V", 0)
+
+    def key_constants():
+        ts(R("ID"), R("IB", 0, 128), R("PIF"), None, OP.is_equal)
+        ts(R("IDN"), R("ID"), -1.0, None, OP.mult)
+        ts(R("O8K"), R("IB", 0, 8), R("GRF"), 16.0, OP.is_equal, OP.mult)
+        ts(R("BB"), R("IB4", 0, 128), R("GRF"), None, OP.is_equal)
+        aff(R("CK"), R("IB15"), -1.0, 15.0)
+
+    def late_constants():
+        aff(R("IDF"), R("ID"), 1.0)
+        aff(R("O8M"), R("O8K"), -0.0625)
+        aff(R("LN16"), R("LNF"), 16.0)
+        aff(R("CIX"), R("CIX"), 1.0, R("LN16"))
+        aff(R("LREV"), R("LNF"), -1.0, 15.0)
+        ts(R("MSKD"), R("IB15"), R("LNF"), None, OP.is_equal)
+        cp(R("LID"), R("IB", 0, 16))
+        ts(R("SEGM"), R("IB15"), 0.0, None, OP.is_gt)
+        ms(R("C37"), 37.0)
+        ms(R("ZR"), 0.0)
+        ms(R("O16"), 0.0625)
+        ms(R("W", 1024, 1280), 0.0)
+        ts(R("NEGM"), R("IB15"), R("LNF"), -2097152.0, OP.not_equal, OP.mult)
+        tt(R("NWN"), R("NWN"), R("NEGM"), OP.add)
+        ts(R("LLN"), R("IB", 0, 16), 0.0, R("LNF"), OP.mult, OP.add)
+        ts(R("BSM"), R("IB15", 0, 128), float(MV), 16384.0, OP.is_ge, OP.mult)
+        tt(R("BSM"), R("BSM"), R("BB"), OP.mult)
+        cp(R("WTF"), R("WTI"))
+        cp(R("KAF"), R("KAI"))
+
+    def score_constants():
+        aff(R("WB"), R("BB"), R("WTF"))
+        aff(R("O8F"), R("O8K"), 0.0625)
+        aff(R("O8W"), R("O8F"), R("WTF"))
+        aff(R("BBF"), R("BB"), 1.0)
+        ts(R("KR"), R("IB4"), R("LNF"), R("KAF"), OP.is_equal, OP.mult)
+        mm(R("pk", 0, 256), R("BBF"), R("KR"), True, True)
+        aff(R("KAX"), R("pk", 0, 256), 1.0)
+        aff(R("O8S"), R("O8K"), 1024.0)
+        aff(R("O8N"), R("O8K"), -1024.0)
+
+    def parent_constants():
+        ts(R("KH"), R("KRW"), 768, None, OP.bitwise_and)
+        ts(R("KL"), R("KRW"), 255, None, OP.bitwise_and)
+        ts(R("KLF"), R("KL"), R("PIF", 0, 1, 1, 2), None, OP.mult)
+        aff(R("KHF"), R("CK", 0, 128, 1, 2), 1024.0)
+        aff(R("OMP"), R("PIF"), -1.0, 1.0)
+        tt(R("KHF"), R("KHF"), R("KH"), OP.add)
+        ts(R("KHF"), R("KHF"), R("OMP", 0, 1, 1, 2), None, OP.mult)
+        tt(R("KC", 0, 128), R("KHF"), R("KLF"), OP.add)
+        aff(R("KC", 128, 256), R("KC", 0, 128), 1.0)
+        ts(R("TRIM"), R("IB15"), R("LNF"), 2097152.0, OP.is_le, OP.mult)
+        aff(R("BB4"), R("BB"), 8192.0)
+        aff(R("TRX"), R("TRX"), 1.0, R("LNF"))
+        aff(R("TRD"), R("TRD"), 1.0, R("LNF"))
+        for c in range(4):
+            aff(R("LP%d" % c), R("LNF"), 1.0, 16.0 - 4 * c)
+        aff(R("NMSK"), R("MSKD"), -1.0, 1.0)
+
+    def room(f, c, rooms, res):
+        o = 1024 * (c % 2)
+        for b in (0, 512):
+            if rooms:
+                mm(R("pd", o + b, o + b + 512), R("IDN" if c else "ID"), R("CX%d" % f, 1024 * c + b, 1024 * c + b + 512), True, not c)
+        for b in (0, 512):
+            if res:
+                mm(R("pd", o + b, o + b + 512), R("ID"), R("DD", 16 + 1024 * c + b, 528 + 1024 * c + b), False, True)
+
+    def set_words():
+        tt(R("TW"), IND(R("W"), R("LST")), R("NMSK"), OP.mult)
+        tt(IND(R("W"), R("LST")), R("TW"), R("NW"), OP.add)
+
+    sent = 0
+    for t in range(1, ROUNDS + 1):
+        f = (t - 1) % PH
+        f2 = t % PH
+        wf, capf = R("W", f, 1024, 4), R("CAPS", f, 1024, 4)
+        if t == 1:
+            win = R("RW", 0, SH + 2304)
+            for c in (0, 1):
+                cp(R("DD", 16 + 1024 * c, 1040 + 1024 * c), IND(win, R("OFFS", 64 * c, 64 * c + 64)))
+            for c in (2, 3):
+                act(R("DD", 16 + 1024 * c, 1040 + 1024 * c), IND(win, R("OFFS", 64 * c, 64 * c + 64)), AF.Copy)
+            key_constants()
+            room(0, 0, True, False)
+            room(0, 1, True, False)
+        mm(R("pk", 0, 256), R("ONE", 0, 128, 1, 1), R("CK", 0, 256, 1, 1), True, False)
+        mm(R("pc", 256, 512), R("ID"), capf, True, True)
+        room(f, 1, False, True)
+        tt(R("X", 0, 1024), R("DD", 16, 1040), R("pd", 0, 1024), OP.max)
+        room(f, 2, True, True)
+        act(R("X", 1024, 2048), R("pd", 1024, 2048), AF.Relu)
+        room(f, 3, True, True)
+        act(R("X", 2048, 3072), R("pd", 0, 1024), AF.Relu)
+        act(R("X", 3072, 4096), R("pd", 1024, 2048), AF.Relu)
+        if t > 1:
+            mm(R("pn", 256, 272), R("IDF"), R("CIX"), True, False)
+        scan(R("E1"), R("DD", 15, 4111), R("SEG"), OP.max, OP.min)
+        tt(R("TT"), R("E1", 15, 4096, 16), R("DD", 31, 4112, 16), OP.max)
+        tt(R("FL"), R("TT"), R("pc", 256, 512), OP.is_gt)
+        scan(R("E2", 0, 4096, -1), R("DD", 17, 4113, -1), R("SEG"), OP.max, OP.min)
+        for h in (0, 1):
+            for k in range(16):
+                mm(R("pk", 128 * h + k, 128 * h + 128, 16), R("X", 2048 * h + k, 2048 * h + 2048, 16), R("O8K"), False, h == 1 and k == 15)
+            if h == 0:
+                mm(R("pb", 0, 256), R("BB"), R("FL"), True, True)
+        if t == 1:
+            late_constants()
+            mm(R("pn", 256, 272), R("IDF"), R("CIX"), True, False)
+        ts(R("pb", 0, 256), R("pb", 0, 256), R("LIM"), -512.0, OP.is_gt, OP.mult)
+        tt(R("MN"), R("TT"), R("pb", 0, 256), OP.add)
+        scan(R("KI"), R("SEGM"), R("pk", 0, 256), OP.mult, OP.max)
+        ts(R("TA"), R("KI", 15, 256, 16), 15, None, OP.bitwise_and)
+        tt(R("EX"), IND(R("TA"), R("LID")), R("MSKD"), OP.mult)
+        cp(R("TAF"), R("TA"))
+        for h in (0, 1):
+            mm(R("pn", 256 + 8 * h, 264 + 8 * h), R("EX", 128 * h, 128 * h + 128), R("O8M"), False, h == 1)
+        act(R("EXP"), IND(R("TAF"), R("LID")), AF.Copy)
+        cp(R("IDX"), R("pn", 256, 272))
+        tt(R("A1"), IND(R("E1"), R("IDX")), R("MN"), OP.max)
+        tt(R("A2"), IND(R("E2"), R("IDX")), R("A1"), OP.max)
+        tt(R("F2"), R("A2"), R("pc", 256, 512), OP.is_gt)
+        mm(R("pn", 0, 256), R("BB"), R("F2"), True, True)
+        ts(R("pn", 0, 256), R("pn", 0, 256), R("LIM"), None, OP.is_le)
+        mo, ld = R("MO%d" % t), R("LD%d" % t)
+        tt(mo, R("A2"), R("pn", 0, 256), OP.mult)
+        dst = T.cores[(rank + 1 + (t - 1) % 7) % 8]
+        ne = len(topo.engines(core, dst))
+        rid, pid, _se = topo.addr(dst)
+        sc["deps"]("G", mo["r"], [])
+        g.remote_dma(ld["ap"], mo["ap"], T.sem["arr%d" % t], T.sem["sent"], pid, rid, topo.mask(core, dst))
+        sent += ne
+        sc["record"]("arr%d" % t, ne, [], ld["w"], None)
+        if t < PH:
+            for k in range(16):
+                widen(t, k, "G")
+        if t == 1:
+            for b in (0, 512):
+                mm(R("pd", 1024 + b, 1536 + b), R("ID"), R("CAPS", b, b + 512), True, False)
+                mm(R("pd", 1024 + b, 1536 + b), R("IDN"), R("RW", SH + b, SH + b + 512), False, True)
+            act(R("SL"), R("pd", 1024, 2048), AF.Relu)
+        for h in (0, 1):
+            mm(R("pd", 128 * h, 128 * h + 128), R("EXP", 128 * h, 128 * h + 128), R("ID"), True, True)
+        mm(R("pd", 512, 768), R("ID"), capf, True, False)
+        mm(R("pd", 512, 768), R("IDN"), mo, False, True)
+        act(R("SL", f, 1024, 4), R("pd", 512, 768), AF.Relu)
+        act(R("RW", SH + f, SH + 1024, 4), mo, AF.Copy)
+        if t == 1:
+            score_constants()
+        else:
+            set_words()
+        ts(R("EQT"), R("pd", 0, 256), R("LREV"), 128.0 * (t + 4), OP.is_equal, OP.mult)
+        tg, b2, sm, bf = R("pb", 256, 512), R("pc", 256, 512), R("pb", 0, 256), R("BRI", f, 1024, 4)
+        tt(tg, R("EQT"), R("pb", 0, 256), OP.mult)
+        if t < ROUNDS:
+            act(R("JK"), R("pb", 0, 256), AF.Copy, scale=-1.0 / 512, acc=R("FC"))
+            mm(R("pc", 0, 1), R("O16"), R("FC"), True, True)
+            aff(R("SC"), R("pc", 0, 1), 1.0)
+            aff(R("H1"), R("SC"), 0.5, 8388608.0)
+            aff(R("H2"), R("H1"), -2.0, 16777216.0)
+            act(R("H1"), R("SC"), AF.Abs, 1.0, R("H2"))
+            aff(R("LIM"), R("H1"), 1.0, 4.0)
+        else:
+            y = R("RW", SH, SH + 1024)
+            sc["dma"]("Y", "oyr", T.yr[:], y["ap"], [], [y])
+        if t == 1:
+            for c in (1, 2, 3):
+                halves(c)
+                code(c, c + 1, R("W", c, 1024, 4), 1 + c % 2)
+        elif t == 2:
+            code(1, 6, R("OFB"), 2)
+
+        def own_words():
+            tt(b2, R("YL", f, 1024, 4), tg, OP.add)
+            if t == 1:
+                tt(bf, bf, b2, OP.min)
+                tt(wf, R("OFA"), tg, OP.add)
+            else:
+                tt(b2, bf, b2, OP.min)
+                ts(sm, wf, 4096.0, None, OP.is_ge)
+                tt(R("DF"), wf, tg, OP.add)
+                tt(R("DF"), R("DF"), b2, OP.subtract)
+                tt(R("DF"), R("DF"), sm, OP.mult)
+                tt(bf if t == 2 else wf, R("DF"), b2, OP.add)
+                if t == 2:
+                    ts(sm, sm, 2097152.0, None, OP.mult)
+                    tt(R("YL", f, 1024, 4), R("YL", f, 1024, 4), sm, OP.max)
+                    tt(R("DF"), R("OFB"), tg, OP.add)
+                    tt(wf, R("DF"), sm, OP.subtract)
+        mm(R("pn", 0, 256), R("ID"), R("NEGM"), True, False)
+        mm(R("pn", 0, 256), R("C37", 0, 128, 1, 1), R("IB", 0, 256, 1, 1), False, False)
+        mm(R("pk", 0, 256), R("ONE", 0, 128, 1, 1), R("ZR", 0, 256, 1, 1), True, False)
+        mm(R("pn", 0, 256), R("WB"), ld, False, True)
+        for h in (0, 1):
+            mm(R("pk", 128 * h, 128 * h + 128), R("LD%d" % t, 128 * h, 128 * h + 128), R("BSM"), False, False)
+        for k in range(4):
+            act(R("MR", 256 * k, 256 * k + 256), ld, AF.Copy)
+        if t < ROUNDS:
+            act(R("RW", SH + 1024 + 256 * (t - 1), SH + 1280 + 256 * (t - 1)), ld, AF.Copy)
+            act(R("RW", AREA0 + AREAD * (t - 1), AREA0 + AREAD * (t - 1) + 256), ld, AF.Copy)
+            if t > 2:
+                act(R("RW", AREA0 + AREAD * (t - 3), AREA0 + AREAD * (t - 3) + 256), R("ZR"), AF.Copy)
+        scan(R("UI"), R("SEGM"), R("pn", 0, 256), OP.mult, OP.max)
+        ts(R("U"), R("UI", 15, 256, 16), 4095, None, OP.bitwise_and)
+        tt(R("U2"), R("U"), R("U"), OP.mult)
+        ts(R("BS"), R("U2"), 5, None, OP.arith_shift_right)
+        tt(R("T1"), IND(R("U"), R("LLN")), R("KAX"), OP.mult)
+        tt(R("PI1"), IND(R("BS"), R("LLN")), R("T1"), OP.add)
+        ts(R("PI2"), R("PI1"), 1023, None, OP.bitwise_and)
+        cp(R("POF"), R("PI2"))
+        for b in range((16 - MV) // 2):
+            mm(R("pd", 512 * b, 512 * b + 512), R("ID"), R("MR", 0, 512), True, False)
+        for h in (0, 1):
+            mm(R("pn", 256 + 8 * h, 264 + 8 * h), R("LD%d" % t, 128 * h, 128 * h + 128), R("O8W"), True, False)
+            mm(R("pn", 256 + 8 * h, 264 + 8 * h), R("IB", 128 * h, 128 * h + 128, 1, 1), R("C37", 0, 8, 1, 1), False, True)
+
+        def keys(m0, n, r):
+            for mc in range(m0, m0 + n):
+                for h in (0, 1):
+                    mm(R("pk", 128 * h + mc, 128 * h + 128, 16), R("X", 256 * mc + 128 * h, 256 * mc + 128 * h + 128), r, False, False)
+        spl = [(m0, min(4, 16 - m0)) for m0 in range(MV, 16, 4)]
+        vpl = [(m0, min(4, MV - m0)) for m0 in range(0, MV, 4)]
+        for m0, n in spl:
+            o = 256 * (m0 - MV)
+            act(R("SG", o, o + 256 * n), IND(R("SL"), R("POF", 16 * m0, 16 * (m0 + n))), AF.Copy)
+        for e, (m0, n) in enumerate(vpl):
+            tt(R("X", 256 * m0, 256 * (m0 + n)), IND(R("SL"), R("POF", 16 * m0, 16 * (m0 + n))), R("MR", 0, 256 * n), OP.min)
+            keys(m0, n, R("O8S"))
+            if e < len(spl):
+                m1, n1 = spl[e]
+                for b in range((m1 - MV) // 2, (m1 - MV + n1) // 2):
+                    mm(R("pd", 512 * b, 512 * b + 512), R("IDN"), R("SG", 512 * b, 512 * b + 512), False, True)
+                act(R("X", 256 * m1, 256 * (m1 + n1)), R("pd", 256 * (m1 - MV), 256 * (m1 - MV + n1)), AF.Relu)
+        for m0, n in spl:
+            keys(m0, n, R("O8N"))
+        if t == 1:
+            parent_constants()
+        mm(R("pk", 0, 256), R("ONE", 0, 128, 1, 2), R("KC"), False, True)
+        act(R("NW"), R("NWN"), AF.Relu, 1.0, float(AREAD * t))
+        if t == 1:
+            code(0, 5, R("OFA"), 3)
+        if t < ROUNDS:
+            cp(R("OFFS"), R("W", f2, 1024, 4))
+            win = R("RW", 0, AREA0 + AREAD * (t - 1) + 256)
+            for c in range(4):
+                act(R("DD", 16 + 1024 * c, 1040 + 1024 * c), IND(win, R("OFFS", 64 * c, 64 * c + 64)), AF.Copy)
+            room(f2, 0, True, False)
+            room(f2, 1, True, False)
+        cp(R("UT0"), R("pn", 256, 272))
+        ts(R("UT"), R("UT0"), 4095, None, OP.bitwise_and)
+        tt(R("UT2"), R("UT"), R("UT"), OP.mult)
+        ts(R("BST"), R("UT2"), 5, None, OP.arith_shift_right)
+        own_words()
+        scan(R("KI"), R("SEGM"), R("pk", 0, 256), OP.mult, OP.max)
+        ts(R("TB"), R("KI", 15, 256, 16), 1023, None, OP.bitwise_and)
+        tt(R("P1"), R("UT"), R("TB"), OP.mult)
+        tt(R("P2"), R("P1"), R("BST"), OP.add)
+        ts(R("PL"), R("P2"), 1023, None, OP.bitwise_and)
+        tt(R("EXD"), IND(R("PL"), R("LID")), R("MSKD"), OP.mult)
+        cp(R("EXN"), IND(R("PL"), R("LID")))
+        for h in (0, 1):
+            mm(R("pc", 8 * h, 8 * h + 8), R("EXD", 128 * h, 128 * h + 128), R("O8F"), True, True)
+        for h in (0, 1):
+            mm(R("pb", 128 * h, 128 * h + 128), R("EXN", 128 * h, 128 * h + 128), R("IDF"), True, True)
+        mm(R("pn", 0, 256), R("ID"), R("NEGM"), True, False)
+        cp(R("PLF"), R("pc", 0, 16))
+        if t < ROUNDS:
+            ts(R("PQ"), R("PLF"), 4.0, R("LP%d" % f2), OP.mult, OP.add)
+            cp(R("PLI"), R("PLF"))
+            ts(R("PL3"), R("PLI"), 3, None, OP.bitwise_and)
+            ts(R("PZ"), R("PL3"), float(f2), 8192.0, OP.not_equal, OP.mult)
+            tt(R("PZ"), R("PQ"), R("PZ"), OP.add)
+        cp(R("PBU"), R("pb", 0, 256))
+        o = 0
+        for q in range(15):
+            n = 240 - 16 * q
+            ts(R("EQ", o, o + n), R("PBU", 256 - n, 256), R("PLF", q, q + 1), None, OP.is_equal)
+            mm(R("pn", 256 - n, 256), R("BB4"), R("EQ", o, o + n), False, q == 14)
+            o += n
+            if q == 1:
+                tt(R("PBF"), R("pb", 0, 256), R("TRIM"), OP.add)
+                tt(R("EQ", 1920, 2176), IND(R("PLF"), R("LID")), R("PBF"), OP.is_equal)
+                mm(R("pn", 0, 256), R("BB4"), R("EQ", 1920, 2176), False, False)
+        scan(R("SX"), R("SEGM"), R("pn", 0, 256), OP.mult, OP.max)
+        if t < ROUNDS:
+            tt(R("L3"), R("SX", 15, 256, 16), R("PZ"), OP.max)
+            tt(R("L4"), R("L3"), R("TRD"), OP.min)
+            cp(R("LSD"), R("L4"))
+            out = IND(R("DD"), R("LSD"))
+            op("V", lambda: g.vector.tensor_copy(out["ap"], ld["ap"]), [out], [ld])
+        tt(R("L1"), R("SX", 15, 256, 16), R("TRX"), OP.min)
+        tt(R("L2"), R("L1"), R("PLF"), OP.max)
+        cp(R("LST"), R("L2"))
+        if t == ROUNDS:
+            set_words()
+
+    y = R("W", 0, 1024)
+    sc["dma"]("Y", "oyb", T.yb[:], y["ap"], [], [y])
+    g.sync.wait_ge(T.sem.oyb, 16)
+    g.sync.wait_ge(T.sem.oyr, 16)
+    for q in ("V", "S", "P", "G"):
+        g.wait_ge(T.sem["s" + q], sc["cnt"][q])
+    g.wait_ge(T.sem.sent, sent)
+    for s in LOADS:
+        g.wait_ge(T.sem[s], 16)

@@ -5,7 +5,7 @@ OP = AluOpType
 AF = ActivationFunctionType
 B16, F32, I32, U16 = "bfloat16", "float32", "int32", "uint16"
 ROUNDS, PH = 6, 4
-MV = 8
+MV = 10
 SH = 16
 AREA0, AREAD = 13312, 4352
 RWN = AREA0 + AREAD * 4 + 256
@@ -21,7 +21,7 @@ def _buf(where, dtype, *names):
 
 _buf("sbuf", B16, ("RW", RWN), ("CAPS", 1024), ("SL", 1024), ("DD", DDN), ("E1", 4096), ("E2", 4096), ("X", 4096), ("SEG", 4096), ("TT", 256), ("FL", 256),
      ("F2", 256), ("MN", 256), ("A1", 256), ("A2", 256), ("EX", 256), ("EXP", 256), ("JK", 256), ("MR", 1024), ("SG", 2048), ("EQ", 2176))
-_buf("sbuf", F32, ("W", 1280), ("BC", 1024), ("OFA", 256), ("OFB", 256), ("EQT", 256), ("DF", 256), ("T1", 256), ("EXD", 256), ("EXN", 256),
+_buf("sbuf", F32, ("W", 1280), ("BC", 1024), ("OFA", 256), ("OFB", 256), ("EQT", 256), ("DF", 256), ("T1", 256), ("EXD", 256), ("EXN", 256), ("PLT", 16), ("SM", 256),
      ("PBF", 256), ("SX", 256), ("S16F", 160), ("TW", 256), ("NW", 256))
 _buf("sbuf", I32, ("BRI", 1024), ("YL", 1024), ("KI", 256), ("S16I", 224), ("UI", 256), ("PI1", 256), ("PI2", 256), ("WTI", 1), ("KAI", 1), ("I1", 8))
 _buf("sbuf", U16, ("OFFS", 256), ("IDX", 16), ("POF", 256), ("PBU", 256), ("LST", 16), ("LSD", 16), ("LID", 16), ("LLN", 16))
@@ -227,8 +227,8 @@ def rank_program(g, core, T, topo):
         ts(R("KI"), R("BRI", f, 1024, 4), 4095, None, OP.bitwise_and)
         ts(R("BC", 256 * f, 256 * f + 256), R("KI"), float(SH), None, OP.add)
 
-    def code(f, t, out, q):
-        a, b = (R("pn", 0, 256), R("pc", 0, 256)) if q == "V" else (R("MN"), R("A1"))
+    def code(f, t, out, q, tiles=None):
+        a, b = (R("pn", 0, 256), R("pc", 0, 256)) if q == "V" else (R(tiles[0]), R(tiles[1]))
         ts(a, R("BRI", f, 1024, 4), float(-65536 * (t - 1)), -8192.0, OP.is_lt, OP.mult)
         ts(b, R("YL", f, 1024, 4), float(4096 * t), -8192.0, OP.is_lt, OP.mult)
         bc = R("BC", 256 * f, 256 * f + 256)
@@ -245,6 +245,11 @@ def rank_program(g, core, T, topo):
         act(R("SEG", n, 2 * n), R("SEG", 0, n), AF.Copy)
     for n in (1024, 2048):
         gcopy(R("SEG", n, 2 * n), R("SEG", 0, n), n)
+    iota(R("C37"), [[0, 128]], 37, 0)
+    iota(R("ZR"), [[0, 256]], 0, 0)
+    iota(R("W", 1024, 1280), [[0, 256]], 0, 0)
+    cp(R("WTF"), R("WTI"))
+    cp(R("KAF"), R("KAI"))
     for k in range(4, 16):
         widen(0, k, "S", 1)
     for k in range(11, 16):
@@ -271,46 +276,43 @@ def rank_program(g, core, T, topo):
         ts(R("MSKD"), R("IB15"), R("LNF"), None, OP.is_equal)
         cp(R("LID"), R("IB", 0, 16))
         ts(R("SEGM"), R("IB15"), 0.0, None, OP.is_gt)
-        ms(R("C37"), 37.0)
-        ms(R("ZR"), 0.0)
-        ms(R("O16"), 0.0625)
-        ms(R("W", 1024, 1280), 0.0)
-        ts(R("NEGM"), R("IB15"), R("LNF"), -2097152.0, OP.not_equal, OP.mult)
-        tt(R("NWN"), R("NWN"), R("NEGM"), OP.add)
-        ts(R("LLN"), R("IB", 0, 16), 0.0, R("LNF"), OP.mult, OP.add)
-        ts(R("BSM"), R("IB15", 0, 128), float(MV), 16384.0, OP.is_ge, OP.mult)
-        tt(R("BSM"), R("BSM"), R("BB"), OP.mult)
-        cp(R("WTF"), R("WTI"))
-        cp(R("KAF"), R("KAI"))
-
-    def score_constants():
+        aff(R("NEGM"), R("MSKD"), 2097152.0, -2097152.0)
+        aff(R("O16"), R("ONE"), 0.0625)
+        aff(R("NMSK"), R("MSKD"), -1.0, 1.0)
+        aff(R("KHF"), R("CK", 0, 128, 1, 2), 1024.0)
+        aff(R("OMP"), R("PIF"), -1.0, 1.0)
+        aff(R("BB4"), R("BB"), 8192.0)
         aff(R("WB"), R("BB"), R("WTF"))
         aff(R("O8F"), R("O8K"), 0.0625)
         aff(R("O8W"), R("O8F"), R("WTF"))
         aff(R("BBF"), R("BB"), 1.0)
-        ts(R("KR"), R("IB4"), R("LNF"), R("KAF"), OP.is_equal, OP.mult)
-        mm(R("pk", 0, 256), R("BBF"), R("KR"), True, True)
-        aff(R("KAX"), R("pk", 0, 256), 1.0)
         aff(R("O8S"), R("O8K"), 1024.0)
         aff(R("O8N"), R("O8K"), -1024.0)
+
+    def score_constants():
+        ts(R("LLN"), R("IB", 0, 16), 0.0, R("LNF"), OP.mult, OP.add)
+        ts(R("BSM"), R("IB15", 0, 128), float(MV), 16384.0, OP.is_ge, OP.mult)
+        ts(R("KR"), R("IB4"), R("LNF"), R("KAF"), OP.is_equal, OP.mult)
+        mm(R("pk", 0, 256), R("BBF"), R("KR"), True, True)
+        tt(R("BSM"), R("BSM"), R("BB"), OP.mult)
+        aff(R("KAX"), R("pk", 0, 256), 1.0)
 
     def parent_constants():
         ts(R("KH"), R("KRW"), 768, None, OP.bitwise_and)
         ts(R("KL"), R("KRW"), 255, None, OP.bitwise_and)
-        ts(R("KLF"), R("KL"), R("PIF", 0, 1, 1, 2), None, OP.mult)
-        aff(R("KHF"), R("CK", 0, 128, 1, 2), 1024.0)
-        aff(R("OMP"), R("PIF"), -1.0, 1.0)
         tt(R("KHF"), R("KHF"), R("KH"), OP.add)
+        ts(R("KLF"), R("KL"), R("PIF", 0, 1, 1, 2), None, OP.mult)
         ts(R("KHF"), R("KHF"), R("OMP", 0, 1, 1, 2), None, OP.mult)
-        tt(R("KC", 0, 128), R("KHF"), R("KLF"), OP.add)
-        aff(R("KC", 128, 256), R("KC", 0, 128), 1.0)
         ts(R("TRIM"), R("IB15"), R("LNF"), 2097152.0, OP.is_le, OP.mult)
-        aff(R("BB4"), R("BB"), 8192.0)
+        tt(R("KC", 0, 128), R("KHF"), R("KLF"), OP.add)
+        tt(R("NWN"), R("NWN"), R("NEGM"), OP.add)
+        cp(R("KC", 128, 256), R("KC", 0, 128))
+
+    def list_constants():
         aff(R("TRX"), R("TRX"), 1.0, R("LNF"))
         aff(R("TRD"), R("TRD"), 1.0, R("LNF"))
         for c in range(4):
             aff(R("LP%d" % c), R("LNF"), 1.0, 16.0 - 4 * c)
-        aff(R("NMSK"), R("MSKD"), -1.0, 1.0)
 
     def room(f, c, rooms, res):
         o = 1024 * (c % 2)
@@ -321,9 +323,11 @@ def rank_program(g, core, T, topo):
             if res:
                 mm(R("pd", o + b, o + b + 512), R("ID"), R("DD", 16 + 1024 * c + b, 528 + 1024 * c + b), False, True)
 
-    def set_words():
-        tt(R("TW"), IND(R("W"), R("LST")), R("NMSK"), OP.mult)
-        tt(IND(R("W"), R("LST")), R("TW"), R("NW"), OP.add)
+    word_steps = [lambda: tt(R("L1"), R("SX", 15, 256, 16), R("TRX"), OP.min),
+                  lambda: tt(R("L2"), R("L1"), R("PLF"), OP.max),
+                  lambda: cp(R("LST"), R("L2")),
+                  lambda: tt(R("TW"), IND(R("W"), R("LST")), R("NMSK"), OP.mult),
+                  lambda: tt(IND(R("W"), R("LST")), R("TW"), R("NW"), OP.add)]
 
     sent = 0
     for t in range(1, ROUNDS + 1):
@@ -343,17 +347,21 @@ def rank_program(g, core, T, topo):
         mm(R("pc", 256, 512), R("ID"), capf, True, True)
         room(f, 1, False, True)
         tt(R("X", 0, 1024), R("DD", 16, 1040), R("pd", 0, 1024), OP.max)
+        mm(R("pn", 0, 256), R("ID"), R("DD", 31, 4112, 16), True, True)
         room(f, 2, True, True)
         act(R("X", 1024, 2048), R("pd", 1024, 2048), AF.Relu)
         room(f, 3, True, True)
         act(R("X", 2048, 3072), R("pd", 0, 1024), AF.Relu)
         act(R("X", 3072, 4096), R("pd", 1024, 2048), AF.Relu)
-        if t > 1:
-            mm(R("pn", 256, 272), R("IDF"), R("CIX"), True, False)
         scan(R("E1"), R("DD", 15, 4111), R("SEG"), OP.max, OP.min)
-        tt(R("TT"), R("E1", 15, 4096, 16), R("DD", 31, 4112, 16), OP.max)
-        tt(R("FL"), R("TT"), R("pc", 256, 512), OP.is_gt)
         scan(R("E2", 0, 4096, -1), R("DD", 17, 4113, -1), R("SEG"), OP.max, OP.min)
+        tt(R("TT"), R("E1", 15, 4096, 16), R("pn", 0, 256), OP.max)
+        if t > 1:
+            word_steps[0]()
+        tt(R("FL"), R("TT"), R("pc", 256, 512), OP.is_gt)
+        if t > 1:
+            word_steps[1]()
+            word_steps[2]()
         for h in (0, 1):
             for k in range(16):
                 mm(R("pk", 128 * h + k, 128 * h + 128, 16), R("X", 2048 * h + k, 2048 * h + 2048, 16), R("O8K"), False, h == 1 and k == 15)
@@ -361,7 +369,7 @@ def rank_program(g, core, T, topo):
                 mm(R("pb", 0, 256), R("BB"), R("FL"), True, True)
         if t == 1:
             late_constants()
-            mm(R("pn", 256, 272), R("IDF"), R("CIX"), True, False)
+        mm(R("pn", 256, 272), R("IDF"), R("CIX"), True, False)
         ts(R("pb", 0, 256), R("pb", 0, 256), R("LIM"), -512.0, OP.is_gt, OP.mult)
         tt(R("MN"), R("TT"), R("pb", 0, 256), OP.add)
         scan(R("KI"), R("SEGM"), R("pk", 0, 256), OP.mult, OP.max)
@@ -403,14 +411,16 @@ def rank_program(g, core, T, topo):
         if t == 1:
             score_constants()
         else:
-            set_words()
+            word_steps[3]()
         ts(R("EQT"), R("pd", 0, 256), R("LREV"), 128.0 * (t + 4), OP.is_equal, OP.mult)
-        tg, b2, sm, bf = R("pb", 256, 512), R("pc", 256, 512), R("pb", 0, 256), R("BRI", f, 1024, 4)
+        if t > 1:
+            word_steps[4]()
+        tg, b2, sm, bf = R("pd", 1536, 1792), R("pd", 1792, 2048), R("SM"), R("BRI", f, 1024, 4)
         tt(tg, R("EQT"), R("pb", 0, 256), OP.mult)
         if t < ROUNDS:
             act(R("JK"), R("pb", 0, 256), AF.Copy, scale=-1.0 / 512, acc=R("FC"))
-            mm(R("pc", 0, 1), R("O16"), R("FC"), True, True)
-            aff(R("SC"), R("pc", 0, 1), 1.0)
+            mm(R("pd", 1024, 1025), R("O16"), R("FC"), True, True)
+            aff(R("SC"), R("pd", 1024, 1025), 1.0)
             aff(R("H1"), R("SC"), 0.5, 8388608.0)
             aff(R("H2"), R("H1"), -2.0, 16777216.0)
             act(R("H1"), R("SC"), AF.Abs, 1.0, R("H2"))
@@ -419,29 +429,28 @@ def rank_program(g, core, T, topo):
             y = R("RW", SH, SH + 1024)
             sc["dma"]("Y", "oyr", T.yr[:], y["ap"], [], [y])
         if t == 1:
-            for c in (1, 2, 3):
+            for c, tiles in ((1, ("MN", "A1")), (2, ("FL", "F2")), (3, ("A2", "EX"))):
                 halves(c)
-                code(c, c + 1, R("W", c, 1024, 4), 1 + c % 2)
-        elif t == 2:
-            code(1, 6, R("OFB"), 2)
-
-        def own_words():
-            tt(b2, R("YL", f, 1024, 4), tg, OP.add)
-            if t == 1:
-                tt(bf, bf, b2, OP.min)
-                tt(wf, R("OFA"), tg, OP.add)
-            else:
-                tt(b2, bf, b2, OP.min)
-                ts(sm, wf, 4096.0, None, OP.is_ge)
-                tt(R("DF"), wf, tg, OP.add)
-                tt(R("DF"), R("DF"), b2, OP.subtract)
-                tt(R("DF"), R("DF"), sm, OP.mult)
-                tt(bf if t == 2 else wf, R("DF"), b2, OP.add)
-                if t == 2:
-                    ts(sm, sm, 2097152.0, None, OP.mult)
-                    tt(R("YL", f, 1024, 4), R("YL", f, 1024, 4), sm, OP.max)
-                    tt(R("DF"), R("OFB"), tg, OP.add)
-                    tt(wf, R("DF"), sm, OP.subtract)
+                code(c, c + 1, R("W", c, 1024, 4), 1 + c % 2, tiles)
+            code(0, 5, R("OFA"), 1, ("MN", "A1"))
+            code(1, 6, R("OFB"), 2, ("FL", "F2"))
+            parent_constants()
+        yf = R("YL", f, 1024, 4)
+        if t > 1:
+            if t < ROUNDS:
+                cp(R("OFFS"), R("W", f2, 1024, 4))
+            tt(b2, yf, tg, OP.add)
+            ts(sm, wf, 4096.0, None, OP.is_ge)
+            tt(b2, bf, b2, OP.min)
+            if t == 2:
+                tt(R("EQT"), R("OFB"), tg, OP.add)
+            own = [lambda: tt(R("DF"), wf, tg, OP.add), lambda: tt(tg, R("DF"), b2, OP.subtract),
+                   lambda: tt(R("DF"), sm, tg, OP.mult), lambda: tt(bf if t == 2 else wf, R("DF"), b2, OP.add)]
+            if t == 2:
+                own += [lambda: ts(sm, sm, 2097152.0, None, OP.mult), lambda: tt(yf, yf, sm, OP.max),
+                        lambda: tt(wf, R("EQT"), sm, OP.subtract)]
+        else:
+            own = [lambda: tt(b2, yf, tg, OP.add), lambda: tt(wf, R("OFA"), tg, OP.add), lambda: tt(bf, bf, b2, OP.min)]
         mm(R("pn", 0, 256), R("ID"), R("NEGM"), True, False)
         mm(R("pn", 0, 256), R("C37", 0, 128, 1, 1), R("IB", 0, 256, 1, 1), False, False)
         mm(R("pk", 0, 256), R("ONE", 0, 128, 1, 1), R("ZR", 0, 256, 1, 1), True, False)
@@ -458,13 +467,15 @@ def rank_program(g, core, T, topo):
         scan(R("UI"), R("SEGM"), R("pn", 0, 256), OP.mult, OP.max)
         ts(R("U"), R("UI", 15, 256, 16), 4095, None, OP.bitwise_and)
         tt(R("U2"), R("U"), R("U"), OP.mult)
-        ts(R("BS"), R("U2"), 5, None, OP.arith_shift_right)
         tt(R("T1"), IND(R("U"), R("LLN")), R("KAX"), OP.mult)
+        ts(R("BS"), R("U2"), 5, None, OP.arith_shift_right)
         tt(R("PI1"), IND(R("BS"), R("LLN")), R("T1"), OP.add)
         ts(R("PI2"), R("PI1"), 1023, None, OP.bitwise_and)
         cp(R("POF"), R("PI2"))
-        for b in range((16 - MV) // 2):
-            mm(R("pd", 512 * b, 512 * b + 512), R("ID"), R("MR", 0, 512), True, False)
+        def pieces(a, b):
+            return [(o, min(512, b - o)) for o in range(a, b, 512)]
+        for o, n in pieces(0, 256 * (16 - MV)):
+            mm(R("pd", o, o + n), R("ID"), R("MR", 0, n), True, False)
         for h in (0, 1):
             mm(R("pn", 256 + 8 * h, 264 + 8 * h), R("LD%d" % t, 128 * h, 128 * h + 128), R("O8W"), True, False)
             mm(R("pn", 256 + 8 * h, 264 + 8 * h), R("IB", 128 * h, 128 * h + 128, 1, 1), R("C37", 0, 8, 1, 1), False, True)
@@ -483,52 +494,62 @@ def rank_program(g, core, T, topo):
             keys(m0, n, R("O8S"))
             if e < len(spl):
                 m1, n1 = spl[e]
-                for b in range((m1 - MV) // 2, (m1 - MV + n1) // 2):
-                    mm(R("pd", 512 * b, 512 * b + 512), R("IDN"), R("SG", 512 * b, 512 * b + 512), False, True)
+                for o, w in pieces(256 * (m1 - MV), 256 * (m1 - MV + n1)):
+                    mm(R("pd", o, o + w), R("IDN"), R("SG", o, o + w), False, True)
                 act(R("X", 256 * m1, 256 * (m1 + n1)), R("pd", 256 * (m1 - MV), 256 * (m1 - MV + n1)), AF.Relu)
         for m0, n in spl:
             keys(m0, n, R("O8N"))
-        if t == 1:
-            parent_constants()
         mm(R("pk", 0, 256), R("ONE", 0, 128, 1, 2), R("KC"), False, True)
         act(R("NW"), R("NWN"), AF.Relu, 1.0, float(AREAD * t))
         if t == 1:
-            code(0, 5, R("OFA"), 3)
-        if t < ROUNDS:
-            cp(R("OFFS"), R("W", f2, 1024, 4))
+            list_constants()
+        def gather(c):
             win = R("RW", 0, AREA0 + AREAD * (t - 1) + 256)
-            for c in range(4):
-                act(R("DD", 16 + 1024 * c, 1040 + 1024 * c), IND(win, R("OFFS", 64 * c, 64 * c + 64)), AF.Copy)
+            act(R("DD", 16 + 1024 * c, 1040 + 1024 * c), IND(win, R("OFFS", 64 * c, 64 * c + 64)), AF.Copy)
+        if t < ROUNDS:
+            if t == 1:
+                cp(R("OFFS"), R("W", f2, 1024, 4))
+            gather(0)
             room(f2, 0, True, False)
-            room(f2, 1, True, False)
-        cp(R("UT0"), R("pn", 256, 272))
-        ts(R("UT"), R("UT0"), 4095, None, OP.bitwise_and)
-        tt(R("UT2"), R("UT"), R("UT"), OP.mult)
-        ts(R("BST"), R("UT2"), 5, None, OP.arith_shift_right)
-        own_words()
+        turned = [lambda: cp(R("UT0"), R("pn", 256, 272)), lambda: ts(R("UT"), R("UT0"), 4095, None, OP.bitwise_and),
+                  lambda: tt(R("UT2"), R("UT"), R("UT"), OP.mult), lambda: ts(R("BST"), R("UT2"), 5, None, OP.arith_shift_right)]
+        for e in range(4):
+            turned[e]()
+            if e < 3:
+                own[e]()
         scan(R("KI"), R("SEGM"), R("pk", 0, 256), OP.mult, OP.max)
         ts(R("TB"), R("KI", 15, 256, 16), 1023, None, OP.bitwise_and)
         tt(R("P1"), R("UT"), R("TB"), OP.mult)
         tt(R("P2"), R("P1"), R("BST"), OP.add)
         ts(R("PL"), R("P2"), 1023, None, OP.bitwise_and)
+        cp(R("PLT"), R("PL"))
         tt(R("EXD"), IND(R("PL"), R("LID")), R("MSKD"), OP.mult)
-        cp(R("EXN"), IND(R("PL"), R("LID")))
+        act(R("EXN"), IND(R("PLT"), R("LID")), AF.Copy)
+        if t < ROUNDS:
+            for c in (1, 2, 3):
+                gather(c)
         for h in (0, 1):
             mm(R("pc", 8 * h, 8 * h + 8), R("EXD", 128 * h, 128 * h + 128), R("O8F"), True, True)
         for h in (0, 1):
             mm(R("pb", 128 * h, 128 * h + 128), R("EXN", 128 * h, 128 * h + 128), R("IDF"), True, True)
         mm(R("pn", 0, 256), R("ID"), R("NEGM"), True, False)
+        for e in own[3:]:
+            e()
+        if t < ROUNDS:
+            room(f2, 1, True, False)
         cp(R("PLF"), R("pc", 0, 16))
         if t < ROUNDS:
+            cp(R("PLI"), R("pc", 0, 16))
             ts(R("PQ"), R("PLF"), 4.0, R("LP%d" % f2), OP.mult, OP.add)
-            cp(R("PLI"), R("PLF"))
             ts(R("PL3"), R("PLI"), 3, None, OP.bitwise_and)
-            ts(R("PZ"), R("PL3"), float(f2), 8192.0, OP.not_equal, OP.mult)
-            tt(R("PZ"), R("PQ"), R("PZ"), OP.add)
         cp(R("PBU"), R("pb", 0, 256))
+        if t < ROUNDS:
+            ts(R("PZ"), R("PL3"), float(f2), 8192.0, OP.not_equal, OP.mult)
         o = 0
         for q in range(15):
             n = 240 - 16 * q
+            if q == 1 and t < ROUNDS:
+                tt(R("PZ"), R("PQ"), R("PZ"), OP.add)
             ts(R("EQ", o, o + n), R("PBU", 256 - n, 256), R("PLF", q, q + 1), None, OP.is_equal)
             mm(R("pn", 256 - n, 256), R("BB4"), R("EQ", o, o + n), False, q == 14)
             o += n
@@ -543,12 +564,8 @@ def rank_program(g, core, T, topo):
             cp(R("LSD"), R("L4"))
             out = IND(R("DD"), R("LSD"))
             op("V", lambda: g.vector.tensor_copy(out["ap"], ld["ap"]), [out], [ld])
-        tt(R("L1"), R("SX", 15, 256, 16), R("TRX"), OP.min)
-        tt(R("L2"), R("L1"), R("PLF"), OP.max)
-        cp(R("LST"), R("L2"))
-        if t == ROUNDS:
-            set_words()
-
+    for step in word_steps:
+        step()
     y = R("W", 0, 1024)
     sc["dma"]("Y", "oyb", T.yb[:], y["ap"], [], [y])
     g.sync.wait_ge(T.sem.oyb, 16)

from concourse.mybir import AluOpType, ActivationFunctionType
import comms_topo

OP = AluOpType
AF = ActivationFunctionType
B16, F32, I32, U16 = "bfloat16", "float32", "int32", "uint16"
ROUNDS, PH = 6, 4
MV = 10
SH = 16
AREA0, AREAD = 13312, 4352
RWN = AREA0 + AREAD * 4 + 256
DDN = 4384

SCRATCH = {}


def _buf(where, dtype, *names):
    for n in names:
        SCRATCH[n[0]] = (where, [128, n[1]], dtype)


_buf("sbuf", B16, ("RW", RWN), ("CAPS", 1024), ("SL", 1024), ("DD", DDN), ("E1", 4096), ("E2", 4096), ("X", 4096), ("SEG", 4096), ("TT", 256), ("FL", 256),
     ("F2", 256), ("MN", 256), ("A1", 256), ("A2", 256), ("EX", 256), ("EXP", 256), ("JK", 256), ("MR", 1024), ("SG", 2048), ("EQ", 2176))
_buf("sbuf", F32, ("W", 1280), ("BC", 1024), ("OFA", 256), ("OFB", 256), ("EQT", 256), ("DF", 256), ("T1", 256), ("EXD", 256), ("EXN", 256), ("PLT", 16), ("SM", 256),
     ("PBF", 256), ("SX", 256), ("S16F", 160), ("TW", 256), ("NW", 256))
_buf("sbuf", I32, ("BRI", 1024), ("YL", 1024), ("KI", 256), ("S16I", 224), ("UI", 256), ("PI1", 256), ("PI2", 256), ("WTI", 1), ("KAI", 1), ("I1", 8))
_buf("sbuf", U16, ("OFFS", 256), ("IDX", 16), ("POF", 256), ("PBU", 256), ("LST", 16), ("LSD", 16), ("LID", 16), ("LLN", 16))
_buf("sbuf", B16, ("IB", 256), ("IB15", 256), ("IB4", 256), ("MSKD", 256), ("NEGM", 256), ("BB", 128), ("BB4", 128), ("WB", 128), ("O8K", 8), ("O8S", 8), ("O8N", 8), ("O8M", 8), ("O8W", 8),
     ("BSM", 128), ("ID", 128), ("IDN", 128), ("CK", 256), ("ONE", 128), ("C37", 128), ("ZR", 256))
_buf("sbuf", F32, ("F1", 24), ("NMSK", 256), ("TRIM", 256), ("SEGM", 256), ("KR", 256), ("KAX", 256), ("BBF", 128), ("O8F", 8), ("CIX", 16), ("TRX", 16), ("TRD", 16), ("IDF", 128), ("O16", 128), ("NWN", 256))
SCRATCH.update({"KRW": ("sbuf", [2, 128], I32), "KH": ("sbuf", [2, 128], I32), "KL": ("sbuf", [2, 128], I32), "KHF": ("sbuf", [2, 128], F32), "KLF": ("sbuf", [2, 128], F32), "KC": ("sbuf", [2, 256], B16)})
_buf("psum", F32, ("pk", 512), ("pb", 512), ("pn", 512), ("pc", 512), ("pd", 2048))
for _f in range(PH):
    _buf("sbuf", B16, ("CX%d" % _f, 4096))
for _r in range(1, ROUNDS + 1):
    _buf("sbuf", B16, ("MO%d" % _r, 256), ("LD%d" % _r, 256))
ALIAS = {n: ("F1", c, 1) for c, n in enumerate(("PIF", "LNF", "GRF", "LREV", "LN16", "OMP", "WTF", "KAF", "LIM", "FC", "SC", "H1", "H2", "LP0", "LP1", "LP2", "LP3"))}
ALIAS.update({n: ("I1", c, 1) for c, n in enumerate(("PIX", "LNI", "GRI"))})
ALIAS.update({n: ("S16I", 16 * c, 16) for c, n in enumerate(("TA", "TB", "U", "U2", "BS", "P2", "PL", "UT0", "UT", "UT2", "BST", "PLI", "PL3"))})
ALIAS.update({n: ("S16F", 16 * c, 16) for c, n in enumerate(("TAF", "P1", "PLF", "L1", "L2", "L3", "L4", "PZ", "PQ"))})
PSUM = ("pk", "pb", "pn", "pc", "pd")
LOADS = ["lcap", "lbr", "lres", "lwt", "lka", "lk0", "lk1"]
SEMAPHORES = ["sV", "sS", "sP", "sG", "sent", "oyr", "oyb"] + LOADS + ["arr%d" % r for r in range(1, ROUNDS + 1)]


def scheduler(g, T):
    eng = {"V": g.vector, "S": g.scalar, "P": g.tensor, "G": g, "Y": g.sync}
    cnt, rec, snap = {}, {}, {}
    clk = {q: {} for q in eng}

    def ref(name, a=None, b=None, s=1, p=None):
        if name in ALIAS:
            name, o, w = ALIAS[name]
            a, b = o + (a or 0), o + (w if b is None else b)
        a = 0 if a is None else a
        b = SCRATCH[name][1][1] if b is None else b
        if s > 0:
            sl = slice(a, b, s)
        else:
            sl = slice(b - 1, a - 1 if a else None, -1)
        rows = slice(0, p) if p else slice(0, SCRATCH[name][1][0])
        x = (name, a, b, max(s, 1), a % max(s, 1))
        return {"ap": T[name][rows, sl], "r": [x], "w": [x]}

    def ind(win, off):
        return {"ap": win["ap"].indirect(off["ap"]), "r": win["r"] + off["r"], "w": win["w"], "x": off["r"]}

    def overlap(q, x, y):
        if x[0] in PSUM and q:
            return x[1] // 512 <= (y[2] - 1) // 512 and y[1] // 512 <= (x[2] - 1) // 512
        if x[3] == y[3] and x[4] != y[4]:
            return False
        return x[1] < y[2] and y[1] < x[2]

    def deps(q, reads, writes):
        need = {}
        for isw, rs in ((False, reads), (True, writes)):
            for x in rs:
                for (y, w, q2, n) in rec.get(x[0], []):
                    same = q2 == q
                    if not overlap(not same, x, y) or (same and q == "P"):
                        continue
                    if not (w or isw or (x[0] in PSUM and not same)):
                        continue
                    if need.get(q2, 0) < n:
                        need[q2] = n
        for q2 in sorted(need):
            n = need[q2]
            if clk[q].get(q2, 0) >= n:
                continue
            if any(q3 != q2 and snap.get((q3, m), {}).get(q2, 0) >= n for q3, m in need.items() if clk[q].get(q3, 0) < m):
                continue
            eng[q].wait_ge(T.sem["s" + q2] if q2 in eng else T.sem[q2], n)
        for q2, n in need.items():
            if clk[q].get(q2, 0) < n:
                clk[q][q2] = n
                for q3, m in snap.get((q2, n), {}).items():
                    if clk[q].get(q3, 0) < m:
                        clk[q][q3] = m

    def record(q, n, reads, writes, by):
        s = dict(clk[by]) if by else {}
        if q in eng:
            s[q] = max(s.get(q, 0), n - 1)
        snap[(q, n)] = s
        for x in writes:
            rec[x[0]] = [e for e in rec.get(x[0], []) if not (x[1] <= e[0][1] and e[0][2] <= x[2] and (x[3] == 1 or x[3:] == e[0][3:]))]
        for w, rs in ((False, reads), (True, writes)):
            for x in rs:
                rec.setdefault(x[0], []).append((x, w, q, n))

    def op(q, fn, outs, ins):
        reads = [x for i in ins for x in i["r"]] + [x for o in outs for x in o.get("x", [])]
        writes = [x for o in outs for x in o["w"]]
        deps(q, reads, writes)
        cnt[q] = cnt.get(q, 0) + 1
        fn().then_inc(T.sem["s" + q], 1)
        record(q, cnt[q], reads, writes, q)

    def dma(q, sem, out, in_, outs, ins):
        reads, writes = [x for i in ins for x in i["r"]], [x for o in outs for x in o["w"]]
        deps(q, reads, writes)
        eng[q].dma_start(out, in_).then_inc(T.sem[sem], 16)
        record(sem, 16, reads, writes, q)

    return {"ref": ref, "ind": ind, "op": op, "dma": dma, "deps": deps, "record": record, "cnt": cnt}


def rank_program(g, core, T, topo):
    rank = T.rank_of(core)
    if rank is None:
        return
    sc = scheduler(g, T)
    R, IND, op = sc["ref"], sc["ind"], sc["op"]

    def val(x):
        return x["ap"] if isinstance(x, dict) else x

    def tt(out, a, b, o):
        op("V", lambda: g.vector.tensor_tensor(out["ap"], a["ap"], b["ap"], o), [out], [a, b])

    def ts(out, a, s1, s2, o0, o1=None):
        ins = [a] + [s for s in (s1, s2) if isinstance(s, dict)]
        if o1 is None:
            op("V", lambda: g.vector.tensor_scalar(out["ap"], a["ap"], val(s1), None, o0), [out], ins)
        else:
            op("V", lambda: g.vector.tensor_scalar(out["ap"], a["ap"], val(s1), val(s2), o0, o1), [out], ins)

    def cp(out, a):
        op("V", lambda: g.vector.tensor_copy(out["ap"], a["ap"]), [out], [a])

    def scan(out, d0, d1, o0, o1):
        op("V", lambda: g.vector.tensor_tensor_scan(out["ap"], d0["ap"], d1["ap"], 0.0, o0, o1), [out], [d0, d1])

    def ms(out, v):
        op("V", lambda: g.vector.memset(out["ap"], v), [out], [])

    def act(out, a, f, scale=1.0, bias=0.0, acc=None):
        ins = [a] + [v for v in (scale, bias) if isinstance(v, dict)]
        if acc:
            op("S", lambda: g.scalar.activation(out["ap"], a["ap"], f, bias=val(bias), scale=val(scale), accum_out=acc["ap"]), [out, acc], ins)
        else:
            op("S", lambda: g.scalar.activation(out["ap"], a["ap"], f, bias=val(bias), scale=val(scale)), [out], ins)

    def aff(out, a, scale, bias=0.0):
        act(out, a, AF.Identity, scale, bias)

    def mm(out, l, r, start, stop):
        op("P", lambda: g.tensor.matmul(out["ap"], l["ap"], r["ap"], start, stop), [out], [l, r])

    def iota(out, pattern, base, cm):
        if SCRATCH[out["r"][0][0]][2] == I32:
            op("G", lambda: g.iota(out["ap"], pattern, base, cm), [out], [])
        else:
            op("G", lambda: g.iota(out["ap"], pattern, base, cm, allow_small_or_imprecise_dtypes=True), [out], [])

    def gcopy(a, b, n):
        op("G", lambda: g.affine_select(a["ap"], b["ap"], [[0, n]], OP.is_gt, 0.0, 1, 0), [a], [b])

    def widen(f, k, q, h=None):
        if h is None:
            a, b = R("CX%d" % f, k, 4096, 16), R("CAPS", f, 1024, 4)
        else:
            a, b = R("CX%d" % f, 2048 * h + k, 2048 * h + 2048, 16), R("CAPS", 512 * h + f, 512 * h + 512, 4)
        if q == "G":
            gcopy(a, b, 256 if h is None else 128)
        elif q == "V":
            cp(a, b)
        else:
            act(a, b, AF.Copy)

    sc["dma"]("Y", "lbr", R("BRI")["ap"], T.br[:], [R("BRI")], [])
    sc["dma"]("S", "lcap", R("CAPS")["ap"], T.cap[:], [R("CAPS")], [])
    x = R("RW", SH, SH + 2304)
    sc["dma"]("Y", "lres", x["ap"], T.res[:], [x], [])
    sc["dma"]("S", "lwt", R("WTI")["ap"], T.wt[:], [R("WTI")], [])
    sc["dma"]("S", "lka", R("KAI")["ap"], T.ka[:], [R("KAI")], [])
    for p in (0, 1):
        g.scalar.dma_start(T.KRW[p:p + 1, :], T.ka[:]).then_inc(T.sem["lk%d" % p], 16)
        sc["record"]("lk%d" % p, 16, [], [("KRW", p, p + 1, 1, 0)], "S")

    iota(R("PIX"), [[0, 1]], 0, 1)
    iota(R("IB15"), [[0, 16], [1, 16]], 0, 0)
    iota(R("IB4"), [[1, 16], [0, 16]], 0, 0)
    iota(R("IB"), [[1, 256]], 0, 0)
    for k in range(4):
        widen(0, k, "G", 1)
    iota(R("CIX"), [[256, 16]], 15, 0)
    iota(R("TRX"), [[16, 16]], 1024, 0)
    iota(R("TRD"), [[16, 16]], 4128, 0)
    iota(R("NWN"), [[1, 256]], AREA0 - AREAD, 0)
    ms(R("RW", 0, SH), 0.0)
    ms(R("DD", 0, 16), 0.0)
    ms(R("DD", 4112, DDN), 0.0)
    ms(R("LIM"), 4.0)
    ms(R("ONE"), 1.0)
    ts(R("LNI"), R("PIX"), 15, None, OP.bitwise_and)
    ts(R("GRI"), R("PIX"), 4, None, OP.arith_shift_right)
    cp(R("PIF"), R("PIX"))
    cp(R("LNF"), R("LNI"))
    cp(R("GRF"), R("GRI"))
    ts(R("SEG", 0, 256), R("IB15"), 0.0, 768.0, OP.is_gt, OP.mult)
    ts(R("SEG", 0, 256), R("SEG", 0, 256), -256.0, None, OP.add)

    def halves(f):
        ts(R("YL", f, 1024, 4), R("BRI", f, 1024, 4), 65535, None, OP.bitwise_and)
        ts(R("KI"), R("BRI", f, 1024, 4), 4095, None, OP.bitwise_and)
        ts(R("BC", 256 * f, 256 * f + 256), R("KI"), float(SH), None, OP.add)

    def code(f, t, out, q, tiles=None):
        a, b = (R("pn", 0, 256), R("pc", 0, 256)) if q == "V" else (R(tiles[0]), R(tiles[1]))
        ts(a, R("BRI", f, 1024, 4), float(-65536 * (t - 1)), -8192.0, OP.is_lt, OP.mult)
        ts(b, R("YL", f, 1024, 4), float(4096 * t), -8192.0, OP.is_lt, OP.mult)
        bc = R("BC", 256 * f, 256 * f + 256)
        if q == "V":
            tt(R("DF"), bc, a, OP.add)
            tt(out, R("DF"), b, OP.add)
        else:
            s = R("pd", 512 * q, 512 * q + 256)
            mm(s, R("IDF"), bc, True, False)
            mm(s, R("ID"), a, False, False)
            mm(s, R("ID"), b, False, True)
            act(out, s, AF.Copy)
    for n in (256, 512):
        act(R("SEG", n, 2 * n), R("SEG", 0, n), AF.Copy)
    for n in (1024, 2048):
        gcopy(R("SEG", n, 2 * n), R("SEG", 0, n), n)
    iota(R("C37"), [[0, 128]], 37, 0)
    iota(R("ZR"), [[0, 256]], 0, 0)
    iota(R("W", 1024, 1280), [[0, 256]], 0, 0)
    cp(R("WTF"), R("WTI"))
    cp(R("KAF"), R("KAI"))
    for k in range(4, 16):
        widen(0, k, "S", 1)
    for k in range(11, 16):
        widen(0, k, "S", 0)
    halves(0)
    code(0, 1, R("W", 0, 1024, 4), "V")
    cp(R("OFFS"), R("W", 0, 1024, 4))
    for k in range(11):
        widen(0, k, "V", 0)

    def key_constants():
        ts(R("ID"), R("IB", 0, 128), R("PIF"), None, OP.is_equal)
        ts(R("IDN"), R("ID"), -1.0, None, OP.mult)
        ts(R("O8K"), R("IB", 0, 8), R("GRF"), 16.0, OP.is_equal, OP.mult)
        ts(R("BB"), R("IB4", 0, 128), R("GRF"), None, OP.is_equal)
        aff(R("CK"), R("IB15"), -1.0, 15.0)

    def late_constants():
        aff(R("IDF"), R("ID"), 1.0)
        aff(R("O8M"), R("O8K"), -0.0625)
        aff(R("LN16"), R("LNF"), 16.0)
        aff(R("CIX"), R("CIX"), 1.0, R("LN16"))
        aff(R("LREV"), R("LNF"), -1.0, 15.0)
        ts(R("MSKD"), R("IB15"), R("LNF"), None, OP.is_equal)
        cp(R("LID"), R("IB", 0, 16))
        ts(R("SEGM"), R("IB15"), 0.0, None, OP.is_gt)
        aff(R("NEGM"), R("MSKD"), 2097152.0, -2097152.0)
        aff(R("O16"), R("ONE"), 0.0625)
        aff(R("NMSK"), R("MSKD"), -1.0, 1.0)
        aff(R("KHF"), R("CK", 0, 128, 1, 2), 1024.0)
        aff(R("OMP"), R("PIF"), -1.0, 1.0)
        aff(R("BB4"), R("BB"), 8192.0)
        aff(R("WB"), R("BB"), R("WTF"))
        aff(R("O8F"), R("O8K"), 0.0625)
        aff(R("O8W"), R("O8F"), R("WTF"))
        aff(R("BBF"), R("BB"), 1.0)
        aff(R("O8S"), R("O8K"), 1024.0)
        aff(R("O8N"), R("O8K"), -1024.0)

    def score_constants():
        ts(R("LLN"), R("IB", 0, 16), 0.0, R("LNF"), OP.mult, OP.add)
        ts(R("BSM"), R("IB15", 0, 128), float(MV), 16384.0, OP.is_ge, OP.mult)
        ts(R("KR"), R("IB4"), R("LNF"), R("KAF"), OP.is_equal, OP.mult)
        mm(R("pk", 0, 256), R("BBF"), R("KR"), True, True)
        tt(R("BSM"), R("BSM"), R("BB"), OP.mult)
        aff(R("KAX"), R("pk", 0, 256), 1.0)

    def parent_constants():
        ts(R("KH"), R("KRW"), 768, None, OP.bitwise_and)
        ts(R("KL"), R("KRW"), 255, None, OP.bitwise_and)
        tt(R("KHF"), R("KHF"), R("KH"), OP.add)
        ts(R("KLF"), R("KL"), R("PIF", 0, 1, 1, 2), None, OP.mult)
        ts(R("KHF"), R("KHF"), R("OMP", 0, 1, 1, 2), None, OP.mult)
        ts(R("TRIM"), R("IB15"), R("LNF"), 2097152.0, OP.is_le, OP.mult)
        tt(R("KC", 0, 128), R("KHF"), R("KLF"), OP.add)
        tt(R("NWN"), R("NWN"), R("NEGM"), OP.add)
        cp(R("KC", 128, 256), R("KC", 0, 128))

    def list_constants():
        aff(R("TRX"), R("TRX"), 1.0, R("LNF"))
        aff(R("TRD"), R("TRD"), 1.0, R("LNF"))
        for c in range(4):
            aff(R("LP%d" % c), R("LNF"), 1.0, 16.0 - 4 * c)

    def room(f, c, rooms, res):
        o = 1024 * (c % 2)
        for b in (0, 512):
            if rooms:
                mm(R("pd", o + b, o + b + 512), R("IDN" if c else "ID"), R("CX%d" % f, 1024 * c + b, 1024 * c + b + 512), True, not c)
        for b in (0, 512):
            if res:
                mm(R("pd", o + b, o + b + 512), R("ID"), R("DD", 16 + 1024 * c + b, 528 + 1024 * c + b), False, True)

    word_steps = [lambda: tt(R("L1"), R("SX", 15, 256, 16), R("TRX"), OP.min),
                  lambda: tt(R("L2"), R("L1"), R("PLF"), OP.max),
                  lambda: cp(R("LST"), R("L2")),
                  lambda: tt(R("TW"), IND(R("W"), R("LST")), R("NMSK"), OP.mult),
                  lambda: tt(IND(R("W"), R("LST")), R("TW"), R("NW"), OP.add)]

    sent = 0
    for t in range(1, ROUNDS + 1):
        f = (t - 1) % PH
        f2 = t % PH
        wf, capf = R("W", f, 1024, 4), R("CAPS", f, 1024, 4)
        if t == 1:
            win = R("RW", 0, SH + 2304)
            for c in (0, 1):
                cp(R("DD", 16 + 1024 * c, 1040 + 1024 * c), IND(win, R("OFFS", 64 * c, 64 * c + 64)))
            for c in (2, 3):
                act(R("DD", 16 + 1024 * c, 1040 + 1024 * c), IND(win, R("OFFS", 64 * c, 64 * c + 64)), AF.Copy)
            key_constants()
            room(0, 0, True, False)
            room(0, 1, True, False)
        mm(R("pk", 0, 256), R("ONE", 0, 128, 1, 1), R("CK", 0, 256, 1, 1), True, False)
        mm(R("pc", 256, 512), R("ID"), capf, True, True)
        room(f, 1, False, True)
        tt(R("X", 0, 1024), R("DD", 16, 1040), R("pd", 0, 1024), OP.max)
        mm(R("pn", 0, 256), R("ID"), R("DD", 31, 4112, 16), True, True)
        room(f, 2, True, True)
        act(R("X", 1024, 2048), R("pd", 1024, 2048), AF.Relu)
        room(f, 3, True, True)
        act(R("X", 2048, 3072), R("pd", 0, 1024), AF.Relu)
        act(R("X", 3072, 4096), R("pd", 1024, 2048), AF.Relu)
        scan(R("E1"), R("DD", 15, 4111), R("SEG"), OP.max, OP.min)
        scan(R("E2", 0, 4096, -1), R("DD", 17, 4113, -1), R("SEG"), OP.max, OP.min)
        tt(R("TT"), R("E1", 15, 4096, 16), R("pn", 0, 256), OP.max)
        if t > 1:
            word_steps[0]()
        tt(R("FL"), R("TT"), R("pc", 256, 512), OP.is_gt)
        if t > 1:
            word_steps[1]()
            word_steps[2]()
        for h in (0, 1):
            for k in range(16):
                mm(R("pk", 128 * h + k, 128 * h + 128, 16), R("X", 2048 * h + k, 2048 * h + 2048, 16), R("O8K"), False, h == 1 and k == 15)
            if h == 0:
                mm(R("pb", 0, 256), R("BB"), R("FL"), True, True)
        if t == 1:
            late_constants()
        mm(R("pn", 256, 272), R("IDF"), R("CIX"), True, False)
        ts(R("pb", 0, 256), R("pb", 0, 256), R("LIM"), -512.0, OP.is_gt, OP.mult)
        tt(R("MN"), R("TT"), R("pb", 0, 256), OP.add)
        scan(R("KI"), R("SEGM"), R("pk", 0, 256), OP.mult, OP.max)
        ts(R("TA"), R("KI", 15, 256, 16), 15, None, OP.bitwise_and)
        tt(R("EX"), IND(R("TA"), R("LID")), R("MSKD"), OP.mult)
        cp(R("TAF"), R("TA"))
        for h in (0, 1):
            mm(R("pn", 256 + 8 * h, 264 + 8 * h), R("EX", 128 * h, 128 * h + 128), R("O8M"), False, h == 1)
        act(R("EXP"), IND(R("TAF"), R("LID")), AF.Copy)
        cp(R("IDX"), R("pn", 256, 272))
        tt(R("A1"), IND(R("E1"), R("IDX")), R("MN"), OP.max)
        tt(R("A2"), IND(R("E2"), R("IDX")), R("A1"), OP.max)
        tt(R("F2"), R("A2"), R("pc", 256, 512), OP.is_gt)
        mm(R("pn", 0, 256), R("BB"), R("F2"), True, True)
        ts(R("pn", 0, 256), R("pn", 0, 256), R("LIM"), None, OP.is_le)
        mo, ld = R("MO%d" % t), R("LD%d" % t)
        tt(mo, R("A2"), R("pn", 0, 256), OP.mult)
        dst = T.cores[(rank + 1 + (t - 1) % 7) % 8]
        ne = len(topo.engines(core, dst))
        rid, pid, _se = topo.addr(dst)
        sc["deps"]("G", mo["r"], [])
        g.remote_dma(ld["ap"], mo["ap"], T.sem["arr%d" % t], T.sem["sent"], pid, rid, topo.mask(core, dst))
        sent += ne
        sc["record"]("arr%d" % t, ne, [], ld["w"], None)
        if t < PH:
            for k in range(16):
                widen(t, k, "G")
        if t == 1:
            for b in (0, 512):
                mm(R("pd", 1024 + b, 1536 + b), R("ID"), R("CAPS", b, b + 512), True, False)
                mm(R("pd", 1024 + b, 1536 + b), R("IDN"), R("RW", SH + b, SH + b + 512), False, True)
            act(R("SL"), R("pd", 1024, 2048), AF.Relu)
        for h in (0, 1):
            mm(R("pd", 128 * h, 128 * h + 128), R("EXP", 128 * h, 128 * h + 128), R("ID"), True, True)
        mm(R("pd", 512, 768), R("ID"), capf, True, False)
        mm(R("pd", 512, 768), R("IDN"), mo, False, True)
        act(R("SL", f, 1024, 4), R("pd", 512, 768), AF.Relu)
        act(R("RW", SH + f, SH + 1024, 4), mo, AF.Copy)
        if t == 1:
            score_constants()
        else:
            word_steps[3]()
        ts(R("EQT"), R("pd", 0, 256), R("LREV"), 128.0 * (t + 4), OP.is_equal, OP.mult)
        if t > 1:
            word_steps[4]()
        tg, b2, sm, bf = R("pd", 1536, 1792), R("pd", 1792, 2048), R("SM"), R("BRI", f, 1024, 4)
        tt(tg, R("EQT"), R("pb", 0, 256), OP.mult)
        if t < ROUNDS:
            act(R("JK"), R("pb", 0, 256), AF.Copy, scale=-1.0 / 512, acc=R("FC"))
            mm(R("pd", 1024, 1025), R("O16"), R("FC"), True, True)
            aff(R("SC"), R("pd", 1024, 1025), 1.0)
            aff(R("H1"), R("SC"), 0.5, 8388608.0)
            aff(R("H2"), R("H1"), -2.0, 16777216.0)
            act(R("H1"), R("SC"), AF.Abs, 1.0, R("H2"))
            aff(R("LIM"), R("H1"), 1.0, 4.0)
        else:
            y = R("RW", SH, SH + 1024)
            sc["dma"]("Y", "oyr", T.yr[:], y["ap"], [], [y])
        if t == 1:
            for c, tiles in ((1, ("MN", "A1")), (2, ("FL", "F2")), (3, ("A2", "EX"))):
                halves(c)
                code(c, c + 1, R("W", c, 1024, 4), 1 + c % 2, tiles)
            code(0, 5, R("OFA"), 1, ("MN", "A1"))
            code(1, 6, R("OFB"), 2, ("FL", "F2"))
            parent_constants()
        yf = R("YL", f, 1024, 4)
        if t > 1:
            if t < ROUNDS:
                cp(R("OFFS"), R("W", f2, 1024, 4))
            tt(b2, yf, tg, OP.add)
            ts(sm, wf, 4096.0, None, OP.is_ge)
            tt(b2, bf, b2, OP.min)
            if t == 2:
                tt(R("EQT"), R("OFB"), tg, OP.add)
            own = [lambda: tt(R("DF"), wf, tg, OP.add), lambda: tt(tg, R("DF"), b2, OP.subtract),
                   lambda: tt(R("DF"), sm, tg, OP.mult), lambda: tt(bf if t == 2 else wf, R("DF"), b2, OP.add)]
            if t == 2:
                own += [lambda: ts(sm, sm, 2097152.0, None, OP.mult), lambda: tt(yf, yf, sm, OP.max),
                        lambda: tt(wf, R("EQT"), sm, OP.subtract)]
        else:
            own = [lambda: tt(b2, yf, tg, OP.add), lambda: tt(wf, R("OFA"), tg, OP.add), lambda: tt(bf, bf, b2, OP.min)]
        mm(R("pn", 0, 256), R("ID"), R("NEGM"), True, False)
        mm(R("pn", 0, 256), R("C37", 0, 128, 1, 1), R("IB", 0, 256, 1, 1), False, False)
        mm(R("pk", 0, 256), R("ONE", 0, 128, 1, 1), R("ZR", 0, 256, 1, 1), True, False)
        mm(R("pn", 0, 256), R("WB"), ld, False, True)
        for h in (0, 1):
            mm(R("pk", 128 * h, 128 * h + 128), R("LD%d" % t, 128 * h, 128 * h + 128), R("BSM"), False, False)
        for k in range(4):
            act(R("MR", 256 * k, 256 * k + 256), ld, AF.Copy)
        if t < ROUNDS:
            act(R("RW", SH + 1024 + 256 * (t - 1), SH + 1280 + 256 * (t - 1)), ld, AF.Copy)
            act(R("RW", AREA0 + AREAD * (t - 1), AREA0 + AREAD * (t - 1) + 256), ld, AF.Copy)
            if t > 2:
                act(R("RW", AREA0 + AREAD * (t - 3), AREA0 + AREAD * (t - 3) + 256), R("ZR"), AF.Copy)
        scan(R("UI"), R("SEGM"), R("pn", 0, 256), OP.mult, OP.max)
        ts(R("U"), R("UI", 15, 256, 16), 4095, None, OP.bitwise_and)
        tt(R("U2"), R("U"), R("U"), OP.mult)
        tt(R("T1"), IND(R("U"), R("LLN")), R("KAX"), OP.mult)
        ts(R("BS"), R("U2"), 5, None, OP.arith_shift_right)
        tt(R("PI1"), IND(R("BS"), R("LLN")), R("T1"), OP.add)
        ts(R("PI2"), R("PI1"), 1023, None, OP.bitwise_and)
        cp(R("POF"), R("PI2"))
        def pieces(a, b):
            return [(o, min(512, b - o)) for o in range(a, b, 512)]
        for o, n in pieces(0, 256 * (16 - MV)):
            mm(R("pd", o, o + n), R("ID"), R("MR", 0, n), True, False)
        for h in (0, 1):
            mm(R("pn", 256 + 8 * h, 264 + 8 * h), R("LD%d" % t, 128 * h, 128 * h + 128), R("O8W"), True, False)
            mm(R("pn", 256 + 8 * h, 264 + 8 * h), R("IB", 128 * h, 128 * h + 128, 1, 1), R("C37", 0, 8, 1, 1), False, True)

        def keys(m0, n, r):
            for mc in range(m0, m0 + n):
                for h in (0, 1):
                    mm(R("pk", 128 * h + mc, 128 * h + 128, 16), R("X", 256 * mc + 128 * h, 256 * mc + 128 * h + 128), r, False, False)
        spl = [(m0, min(4, 16 - m0)) for m0 in range(MV, 16, 4)]
        vpl = [(m0, min(4, MV - m0)) for m0 in range(0, MV, 4)]
        for m0, n in spl:
            o = 256 * (m0 - MV)
            act(R("SG", o, o + 256 * n), IND(R("SL"), R("POF", 16 * m0, 16 * (m0 + n))), AF.Copy)
        for e, (m0, n) in enumerate(vpl):
            tt(R("X", 256 * m0, 256 * (m0 + n)), IND(R("SL"), R("POF", 16 * m0, 16 * (m0 + n))), R("MR", 0, 256 * n), OP.min)
            keys(m0, n, R("O8S"))
            if e < len(spl):
                m1, n1 = spl[e]
                for o, w in pieces(256 * (m1 - MV), 256 * (m1 - MV + n1)):
                    mm(R("pd", o, o + w), R("IDN"), R("SG", o, o + w), False, True)
                act(R("X", 256 * m1, 256 * (m1 + n1)), R("pd", 256 * (m1 - MV), 256 * (m1 - MV + n1)), AF.Relu)
        for m0, n in spl:
            keys(m0, n, R("O8N"))
        mm(R("pk", 0, 256), R("ONE", 0, 128, 1, 2), R("KC"), False, True)
        act(R("NW"), R("NWN"), AF.Relu, 1.0, float(AREAD * t))
        if t == 1:
            list_constants()
        def gather(c):
            win = R("RW", 0, AREA0 + AREAD * (t - 1) + 256)
            act(R("DD", 16 + 1024 * c, 1040 + 1024 * c), IND(win, R("OFFS", 64 * c, 64 * c + 64)), AF.Copy)
        if t < ROUNDS:
            if t == 1:
                cp(R("OFFS"), R("W", f2, 1024, 4))
            gather(0)
            room(f2, 0, True, False)
        turned = [lambda: cp(R("UT0"), R("pn", 256, 272)), lambda: ts(R("UT"), R("UT0"), 4095, None, OP.bitwise_and),
                  lambda: tt(R("UT2"), R("UT"), R("UT"), OP.mult), lambda: ts(R("BST"), R("UT2"), 5, None, OP.arith_shift_right)]
        for e in range(4):
            turned[e]()
            if e < 3:
                own[e]()
        scan(R("KI"), R("SEGM"), R("pk", 0, 256), OP.mult, OP.max)
        ts(R("TB"), R("KI", 15, 256, 16), 1023, None, OP.bitwise_and)
        tt(R("P1"), R("UT"), R("TB"), OP.mult)
        tt(R("P2"), R("P1"), R("BST"), OP.add)
        ts(R("PL"), R("P2"), 1023, None, OP.bitwise_and)
        cp(R("PLT"), R("PL"))
        tt(R("EXD"), IND(R("PL"), R("LID")), R("MSKD"), OP.mult)
        act(R("EXN"), IND(R("PLT"), R("LID")), AF.Copy)
        if t < ROUNDS:
            for c in (1, 2, 3):
                gather(c)
        for h in (0, 1):
            mm(R("pc", 8 * h, 8 * h + 8), R("EXD", 128 * h, 128 * h + 128), R("O8F"), True, True)
        for h in (0, 1):
            mm(R("pb", 128 * h, 128 * h + 128), R("EXN", 128 * h, 128 * h + 128), R("IDF"), True, True)
        mm(R("pn", 0, 256), R("ID"), R("NEGM"), True, False)
        for e in own[3:]:
            e()
        if t < ROUNDS:
            room(f2, 1, True, False)
        cp(R("PLF"), R("pc", 0, 16))
        if t < ROUNDS:
            cp(R("PLI"), R("pc", 0, 16))
            ts(R("PQ"), R("PLF"), 4.0, R("LP%d" % f2), OP.mult, OP.add)
            ts(R("PL3"), R("PLI"), 3, None, OP.bitwise_and)
        cp(R("PBU"), R("pb", 0, 256))
        if t < ROUNDS:
            ts(R("PZ"), R("PL3"), float(f2), 8192.0, OP.not_equal, OP.mult)
        o = 0
        for q in range(15):
            n = 240 - 16 * q
            if q == 1 and t < ROUNDS:
                tt(R("PZ"), R("PQ"), R("PZ"), OP.add)
            ts(R("EQ", o, o + n), R("PBU", 256 - n, 256), R("PLF", q, q + 1), None, OP.is_equal)
            mm(R("pn", 256 - n, 256), R("BB4"), R("EQ", o, o + n), False, q == 14)
            o += n
            if q == 1:
                tt(R("PBF"), R("pb", 0, 256), R("TRIM"), OP.add)
                tt(R("EQ", 1920, 2176), IND(R("PLF"), R("LID")), R("PBF"), OP.is_equal)
                mm(R("pn", 0, 256), R("BB4"), R("EQ", 1920, 2176), False, False)
        scan(R("SX"), R("SEGM"), R("pn", 0, 256), OP.mult, OP.max)
        if t < ROUNDS:
            tt(R("L3"), R("SX", 15, 256, 16), R("PZ"), OP.max)
            tt(R("L4"), R("L3"), R("TRD"), OP.min)
            cp(R("LSD"), R("L4"))
            out = IND(R("DD"), R("LSD"))
            op("V", lambda: g.vector.tensor_copy(out["ap"], ld["ap"]), [out], [ld])
    for step in word_steps:
        step()
    y = R("W", 0, 1024)
    sc["dma"]("Y", "oyb", T.yb[:], y["ap"], [], [y])
    g.sync.wait_ge(T.sem.oyb, 16)
    g.sync.wait_ge(T.sem.oyr, 16)
    for q in ("V", "S", "P", "G"):
        g.wait_ge(T.sem["s" + q], sc["cnt"][q])
    g.wait_ge(T.sem.sent, sent)
    for s in LOADS:
        g.wait_ge(T.sem[s], 16)
